import numpy as np
import ml_dtypes


def mxq(x, axis, fmt="e4m3"):
    dtype, down = {"e4m3": (ml_dtypes.float8_e4m3fn, 7), "e5m2": (ml_dtypes.float8_e5m2, 14)}[fmt]
    v = np.moveaxis(np.asarray(x, np.float32).astype(ml_dtypes.bfloat16).astype(np.float64), axis, -1)
    blocks = v.reshape(v.shape[:-1] + (-1, 32))
    amax = np.abs(blocks).max(-1, keepdims=True)
    byte = np.maximum(np.where(amax > 0, np.frexp(amax)[1] - 1 + 127, 0) - down, 1)
    scale = np.exp2(byte - 127.0)
    codes = (blocks / scale).astype(np.float32).astype(dtype).astype(np.float64)
    return np.moveaxis((codes * scale).reshape(v.shape), -1, axis)


WIDE = False


def mx_kscale(k):
    if not WIDE:
        return np.ones(k)
    levels = np.array([10, -10, 5, -5, 0])
    if k % 512:
        return np.exp2(np.random.permutation(np.resize(levels, k // 32))).repeat(32)
    a = np.empty((k // 512, 16))
    for p in range(k // 512):
        a[p, :8] = np.random.permutation(np.resize(levels, 8))
        for g in range(8):
            far = levels[np.abs(levels - a[p, g]) >= 10]
            a[p, g + 8] = far[np.random.randint(len(far))]
    return np.exp2(a.ravel()).repeat(32)


BF16 = ml_dtypes.bfloat16


def bf(x):
    return np.asarray(x, np.float32).astype(BF16)


def f64(x):
    return np.asarray(x).astype(np.float64)

def planes(Y):
    n, m = Y.shape
    b = f64(bf(Y)).reshape(n // 32, 32, m)
    amax = np.abs(b).max(1)
    byte = np.clip(np.where(amax > 0, np.frexp(amax)[1] - 1 + 127 - 7, 1), 1, 254)
    codes = (b * np.exp2(127.0 - byte)[:, None, :]).reshape(n, m).astype(np.float32).astype(ml_dtypes.float8_e4m3fn).view(np.uint8)
    words = codes.reshape(n // 512, 128, 4, m).transpose(0, 1, 3, 2)
    return np.ascontiguousarray(words), np.ascontiguousarray(byte.astype(np.uint8).reshape(n // 512, 16, m))


F, K, N = 2, 512, 1024


def setup_inputs():
    s, t = mx_kscale(N), mx_kscale(K)
    h0 = np.random.standard_normal((F, K, N)) / np.sqrt(N)
    v0 = np.random.standard_normal((F, N, K)) * np.sqrt(5.0 / K) + 0.4 * np.swapaxes(h0, 1, 2)
    hul0 = np.random.standard_normal((F, K, N))
    u0 = np.random.standard_normal((F, K)) * 0.5
    a0 = 1.0 + 0.1 * np.random.standard_normal((F, K))
    s20 = np.random.uniform(0.5, 1.5, (F, K))
    return {"h": bf(h0 * s), "v": bf(v0 / s[:, None]), "hul": bf(hul0 / t[:, None]),
            "u": bf(u0), "a": bf(a0 * t), "s2": bf(s20)}


def _mse_weight(p, c, u, s2):
    s = np.sum(p * p, axis=2)
    mse = 1.0 - 2.0 * u * c + u * u * (s + s2)
    return 1.0 / mse


def core(h, v, hul, u, a, s2):
    h, v, u, a, s2 = f64(h), f64(v), f64(u), f64(a), f64(s2)
    hul_t = np.swapaxes(f64(hul), 1, 2)
    p = mxq(h, 2, "e4m3") @ mxq(v, 1, "e4m3")
    c = np.sum(h * np.swapaxes(v, 1, 2), axis=2)
    w = _mse_weight(p, c, u, s2)
    e = (a * w * (u * u))[:, :, None] * p
    d1 = mxq(hul_t, 2, "e4m3") @ mxq(e, 1, "e4m3")
    g = a * w * u
    return d1 - hul_t * g[:, None, :]


def reference(h, v, hul, u, a, s2):
    R_out = core(h, v, hul, u, a, s2)
    words, scales = planes(np.moveaxis(R_out, 1, 0).reshape(1024, -1))
    return R_out, words, scales

@@ -1,0 +1,486 @@
+from contextlib import ExitStack
+
+import concourse.mybir as mybir
+from concourse.masks import make_identity
+
+F, K, N = 2, 512, 1024
+FLOPS = 2 * F * 2 * K * K * N
+
+F32 = mybir.dt.float32
+BF16 = mybir.dt.bfloat16
+I32 = mybir.dt.int32
+U32 = mybir.dt.uint32
+U8 = mybir.dt.uint8
+FP8X4 = mybir.dt.float8_e4m3fn_x4
+ALU = mybir.AluOpType
+ACT = mybir.ActivationFunctionType
+
+P = 128
+G = N // 512
+LAST = 1
+C_ON_TENSOR = [(0, 0), (0, 1), (0, 2), (0, 3), (1, 0), (1, 1)]
+
+
+def tile_wmmseunmatcheduplinkgradientsurrogate_kernel(tc, h, v, hul, u, a, s2, out_0, out_1, out_2):
+    nc = tc.nc
+    with ExitStack() as ctx:
+        sb = ctx.enter_context(tc.tile_pool(name="sb", bufs=1))
+        ps = ctx.enter_context(tc.psum_pool(name="ps", bufs=1))
+        ctx.enter_context(tc.manual_schedule())
+
+        def per_f(name, shape, dtype):
+            return [sb.tile(shape, dtype, name=f"{name}{f}", align_bytes=64) for f in range(F)]
+
+        def bank(b, name):
+            return ps.tile([P, 512], F32, name=name, tag=f"bank{b}")
+
+        ident = sb.tile([P, P], F32, name="ident")
+        u_bf = sb.tile([P, F, 4], BF16, name="u_bf")
+        a_bf = sb.tile([P, F, 4], BF16, name="a_bf")
+        s2_bf = sb.tile([P, F, 4], BF16, name="s2_bf")
+        u32 = sb.tile([P, F, 4], F32, name="u32")
+        usq = sb.tile([P, F, 4], F32, name="usq")
+        m2u = sb.tile([P, F, 4], F32, name="m2u")
+        coef = sb.tile([P, F, 2, 4], F32, name="coef")
+        terms = sb.tile([P, F, 4, 8], F32, name="terms")
+        mse = per_f("mse", [P, 4], F32)
+        w = per_f("w", [P, 4], F32)
+        gains = per_f("gains", [P, 2, 4], F32)
+        junk_v = sb.tile([P, 4, 256], F32, name="junk_v")
+        junk_s = sb.tile([P, 4, P], BF16, name="junk_s")
+
+        h_sb = per_f("h_sb", [P, 4, N], BF16)
+        v_sb = per_f("v_sb", [P, G, 4, K], BF16)
+        hul_sb = per_f("hul_sb", [P, 4, N], BF16)
+        h_il = per_f("h_il", [P, G, K, 4], BF16)
+        v_il = per_f("v_il", [P, G, K, 4], BF16)
+        hul_il = per_f("hul_il", [P, N, 4], BF16)
+        e_il = per_f("e_il", [P, K, 4], BF16)
+        h_q, h_s = per_f("h_q", [P, G, K], U32), per_f("h_s", [P, G, K], U8)
+        v_q, v_s = per_f("v_q", [P, G, K], U32), per_f("v_s", [P, G, K], U8)
+        hul_q, hul_s = per_f("hul_q", [P, N], U32), per_f("hul_s", [P, N], U8)
+        e_q, e_s = per_f("e_q", [P, K], U32), per_f("e_s", [P, K], U8)
+        d_q = per_f("d_q", [P, G, K], U32)
+        d_s = sb.tile([P, G, F * K], U8, name="d_s", align_bytes=64)
+        live = {}
+
+        def quantize(codes, scales, src):
+            nc.vector.quantize_mx(out=codes.bitcast(FP8X4), scales=scales, in_=src.rearrange("p c t -> p (c t)"))
+
+        def interleave(eng, dst, src):
+            dst4 = dst.rearrange("p (c i) t -> p c t i", i=4)
+            src4 = src.rearrange("p t (c i) -> p c t i", i=4)
+            if eng == "v":
+                nc.vector.tensor_copy(out=dst4, in_=src4)
+            elif eng == "s":
+                nc.scalar.copy(out=dst4, in_=src4)
+            else:
+                nc.gpsimd.tensor_scalar(out=dst4, in0=src4, scalar1=1.0, scalar2=1.0, op0=ALU.mult, op1=ALU.mult)
+
+        def load_v(f, g):
+            nc.sync.dma_start(out=v_sb[f][:, g], in_=v[f, 512 * g : 512 * (g + 1), :].rearrange("(p t) j -> p t j", t=4))
+
+        def load_h(f, rp):
+            rows = h[f].rearrange("(p r) n -> p r n", r=4)
+            nc.sync.dma_start(out=h_sb[f][:, 2 * rp : 2 * rp + 2, :], in_=rows[:, 2 * rp : 2 * rp + 2, :])
+
+        def load_hul(f, g):
+            cols = slice(512 * g, 512 * (g + 1))
+            nc.sync.dma_start(out=hul_sb[f][:, :, cols], in_=hul[f].rearrange("(p r) n -> p r n", r=4)[:, :, cols])
+
+        def load_vectors():
+            for dst, src in ((u_bf, u), (a_bf, a), (s2_bf, s2)):
+                nc.scalar.dma_start(out=dst[:], in_=src.rearrange("f (p r) -> p f r", r=4))
+
+        def user_square():
+            nc.scalar.activation(out=usq[:], in_=u_bf[:], func=ACT.Square)
+
+        def user_terms():
+            nc.vector.memset(terms[:, :, :, 1], 1.0)
+            nc.vector.tensor_copy(out=u32[:], in_=u_bf[:])
+            nc.vector.tensor_scalar(out=m2u[:], in0=u_bf[:], scalar1=-2.0, scalar2=None, op0=ALU.mult)
+            nc.vector.scalar_tensor_tensor(out=coef[:, :, 1, :], in0=a_bf[:], scalar=-1.0, in1=u_bf[:], op0=ALU.mult, op1=ALU.mult)
+            nc.vector.tensor_tensor(out=coef[:, :, 0, :], in0=a_bf[:], in1=usq[:], op=ALU.mult)
+            nc.vector.tensor_tensor(out=terms[:, :, :, 0], in0=s2_bf[:], in1=usq[:], op=ALU.mult)
+
+        def il_v(eng, f, g, lo=0, hi=K):
+            interleave(eng, v_il[f][:, g, lo:hi, :], v_sb[f][:, g, :, lo:hi])
+
+        def q_v(f, g, lo=0, hi=K):
+            quantize(v_q[f][:, g, lo:hi], v_s[f][:, g, lo:hi], v_il[f][:, g, lo:hi, :])
+
+        def il_hul(eng, f, lo, hi):
+            interleave(eng, hul_il[f][:, lo:hi, :], hul_sb[f][:, :, lo:hi])
+
+        def q_hul(f, g):
+            cols = slice(512 * g, 512 * (g + 1))
+            quantize(hul_q[f][:, cols], hul_s[f][:, cols], hul_il[f][:, cols, :])
+
+        def turn_h(f, rp, g, b):
+            acc = bank(b, f"ht{f}{rp}{g}")
+            live["ht", f, rp, g] = acc
+            for rr in range(2):
+                words = h_sb[f][:, 2 * rp + rr, :].bitcast(F32)
+                for half in range(2):
+                    slot = 2 * rr + half
+                    nc.tensor.transpose(acc[:, P * slot : P * (slot + 1)], words[:, 256 * g + half : 256 * (g + 1) : 2], ident[:])
+
+        def copy_h(eng, f, rp, g):
+            dst = h_il[f][:, g, 256 * rp : 256 * (rp + 1), :].rearrange("p k t -> p (k t)").bitcast(F32)
+            copy = nc.vector.tensor_copy if eng == "v" else nc.scalar.copy
+            copy(out=dst.rearrange("p (r m w) -> p r m w", r=2, w=2),
+                 in_=live["ht", f, rp, g][:].rearrange("p (r w m) -> p r m w", r=2, w=2))
+
+        def q_h(f, rp, g):
+            cols = slice(256 * rp, 256 * (rp + 1))
+            quantize(h_q[f][:, g, cols], h_s[f][:, g, cols], h_il[f][:, g, cols, :])
+
+        def turn_v(f, b):
+            acc = bank(b, f"vt{f}")
+            live["vt", f] = acc
+            for tt in range(2):
+                words = v_sb[f][:, 1, 2 + tt, :].bitcast(F32)
+                for half in range(2):
+                    slot = 2 * tt + half
+                    nc.tensor.transpose(acc[:, P * slot : P * (slot + 1)], words[:, half::2], ident[:])
+
+        def c_vector(f, r):
+            vt = live["vt", f][:].bitcast(BF16).rearrange("p (t w i e) -> p t w i e", t=2, w=2, e=2)
+            hr = h_sb[f][:, r, 512:].rearrange("p (i t) -> p t i", t=4)
+            nc.vector.scalar_tensor_tensor(
+                out=junk_v[:, r, :].rearrange("p (t i) -> p t i", t=2), in0=vt[:, :, r // 2, :, r % 2],
+                scalar=m2u[:, f, r : r + 1], in1=hr[:, 2:4, :], op0=ALU.mult, op1=ALU.mult,
+                accum_out=terms[:, f, r, 2:3])
+
+        def c_tensor(f, r, b):
+            if ("c", f) not in live:
+                live["c", f] = bank(b, f"c{f}")
+            acc = live["c", f]
+            for n, (g, t) in enumerate(C_ON_TENSOR):
+                nc.tensor.matmul(acc[:, P * r : P * (r + 1)], lhsT=h_il[f][:, g, P * r : P * (r + 1), t],
+                                 rhs=v_sb[f][:, g, t, r::4], start=n == 0, stop=n == len(C_ON_TENSOR) - 1)
+
+        def c_diagonal(f, r):
+            nc.vector.scalar_tensor_tensor(
+                out=junk_v[:, r, :P], in0=live["c", f][:, P * r : P * (r + 1)], scalar=m2u[:, f, r : r + 1],
+                in1=ident[:], op0=ALU.mult, op1=ALU.mult, accum_out=terms[:, f, r, 3:4])
+
+        def gains_product(f, jb, b):
+            acc = bank(b, f"p{f}{jb}")
+            live["p", f, jb] = acc
+            jc = slice(P * jb, P * (jb + 1))
+            for r in range(4):
+                kc = slice(P * r, P * (r + 1))
+                for g in range(G):
+                    nc.tensor.matmul_mx(out=acc[:, kc], lhsT=h_q[f][:, g, kc].bitcast(FP8X4), lhsT_scale=h_s[f][:, g, kc],
+                                        rhs=v_q[f][:, g, jc].bitcast(FP8X4), rhs_scale=v_s[f][:, g, jc],
+                                        start=g == 0, stop=g == G - 1)
+
+        def power(f, jb):
+            for r in range(4):
+                nc.scalar.activation(out=junk_s[:, r, :], in_=live["p", f, jb][:, P * r : P * (r + 1)], func=ACT.Square,
+                                     scale=u32[:, f, r : r + 1], accum_out=terms[:, f, r, 4 + jb : 5 + jb])
+
+        def weights_sum(f):
+            nc.vector.tensor_reduce(out=mse[f][:], in_=terms[:, f], axis=mybir.AxisListType.X, op=ALU.add)
+
+        def weights_inverse(f):
+            nc.vector.reciprocal(out=w[f][:], in_=mse[f][:])
+
+        def weights_gains(f):
+            nc.vector.tensor_tensor(out=gains[f][:], in0=coef[:, f], in1=w[f][:].unsqueeze(1).to_broadcast([P, 2, 4]), op=ALU.mult)
+
+        def scale_e(f, jb):
+            dst = e_il[f][:].rearrange("p (s b l) r -> p s b l r", s=4, b=4)[:, :, jb]
+            src = live["p", f, jb][:].rearrange("p (r l s) -> p s l r", r=4, s=4)
+            alpha = gains[f][:, 0, :].unsqueeze(1).unsqueeze(1).to_broadcast([P, 4, 32, 4])
+            nc.vector.tensor_tensor(out=dst, in0=src, in1=alpha, op=ALU.mult)
+
+        def q_e(f, half):
+            cols = slice(256 * half, 256 * (half + 1))
+            quantize(e_q[f][:, cols], e_s[f][:, cols], e_il[f][:, cols, :])
+
+        def back_product(f, g, r, b):
+            acc = bank(b, f"d1{f}{g}{r}")
+            live["d1", f, g, r] = acc
+            jc, nc_ = slice(P * r, P * (r + 1)), slice(512 * g, 512 * (g + 1))
+            nc.tensor.matmul_mx(out=acc[:], lhsT=e_q[f][:, jc].bitcast(FP8X4), lhsT_scale=e_s[f][:, jc],
+                                rhs=hul_q[f][:, nc_].bitcast(FP8X4), rhs_scale=hul_s[f][:, nc_], start=True, stop=True)
+
+        def subtract(f, g, r, lo, hi):
+            if ("dt", f, g) not in live:
+                tag = f"dt{g}" if f == 0 else ("v_il0", "h_il0")[g]
+                live["dt", f, g] = sb.tile([P, 4, 512], F32, name=f"dt{f}{g}", tag=tag, align_bytes=64)
+            nc.vector.scalar_tensor_tensor(
+                out=live["dt", f, g][:, r, :].rearrange("p (t i) -> p t i", t=4)[:, lo:hi],
+                in0=hul_sb[f][:, r, 512 * g : 512 * (g + 1)].rearrange("p (i t) -> p t i", t=4)[:, lo:hi],
+                scalar=gains[f][:, 1, r : r + 1], in1=live["d1", f, g, r][:].rearrange("p (i t) -> p t i", t=4)[:, lo:hi],
+                op0=ALU.mult, op1=ALU.add)
+
+        def turn_d(f, g, t, b):
+            acc = bank(b, f"d{f}{g}{t}")
+            live["d", f, g, t] = acc
+            for r in range(4):
+                nc.tensor.transpose(acc[:, P * r : P * (r + 1)], live["dt", f, g][:, r, P * t : P * (t + 1)], ident[:])
+
+        def copy_d(eng, f, g, t):
+            if ("dsb", f, g) not in live:
+                live["dsb", f, g] = sb.tile([P, 4, K], F32, name=f"dsb{f}{g}")
+            dst = live["dsb", f, g][:, t, :].rearrange("p (m r) -> p m r", r=4)
+            src = live["d", f, g, t][:].rearrange("p (r m) -> p m r", r=4)
+            if eng == "v":
+                nc.vector.tensor_copy(out=dst, in_=src)
+            else:
+                nc.scalar.copy(out=dst, in_=src)
+
+        def store_d(f, g, lo, hi):
+            rows = out_0[f, 512 * g : 512 * (g + 1), :].rearrange("(p t) j -> p t j", t=4)
+            nc.sync.dma_start(out=rows[:, lo:hi, :], in_=live["dsb", f, g][:, lo:hi, :])
+
+        def il_d(eng, f, g, lo=0, hi=K):
+            if ("dil", f, g) not in live:
+                live["dil", f, g] = sb.tile([P, K, 4], BF16, name=f"dil{f}{g}", align_bytes=64)
+            interleave(eng, live["dil", f, g][:, lo:hi, :], live["dsb", f, g][:, :, lo:hi])
+
+        def q_d(f, g, lo=0, hi=K):
+            quantize(d_q[f][:, g, lo:hi], d_s[:, g, K * f + lo : K * f + hi], live["dil", f, g][:, lo:hi, :])
+
+        def store_codes(f, g):
+            words = out_1[g].rearrange("p m t -> p (m t)").bitcast(I32)
+            nc.sync.dma_start(out=words[:, K * f : K * (f + 1)], in_=d_q[f][:, g, :].bitcast(I32))
+
+        def store_scales(g):
+            queues = (nc.sync, nc.scalar, nc.sync, nc.scalar) if g == LAST else (nc.sync,) * 4
+            for q in range(4):
+                queues[q].dma_start(out=out_2[g, 4 * q : 4 * q + 4, :].bitcast(I32), in_=d_s[32 * q : 32 * q + 4, g, :].bitcast(I32))
+
+        load_vectors()
+        make_identity(nc, ident[:])
+        user_square()
+        load_v(0, 1)
+        load_h(0, 0)
+        turn_v(0, 4)
+        il_v("v", 0, 1, 0, 256)
+        turn_h(0, 0, 1, 3)
+        il_v("s", 0, 1, 256, 512)
+        user_terms()
+        q_v(0, 1, 0, 256)
+        copy_h("s", 0, 0, 1)
+        c_vector(0, 1)
+        c_vector(0, 0)
+        load_h(0, 1)
+        turn_h(0, 0, 0, 7)
+        copy_h("s", 0, 0, 0)
+        turn_h(0, 1, 0, 6)
+        load_v(0, 0)
+        copy_h("s", 0, 1, 0)
+        turn_h(0, 1, 1, 1)
+        q_v(0, 1, 256, 512)
+        c_vector(0, 2)
+        load_v(1, 1)
+        load_h(1, 1)
+        load_hul(0, 1)
+        c_vector(0, 3)
+        c_tensor(0, 1, 3)
+        c_tensor(0, 0, 3)
+        copy_h("s", 0, 1, 1)
+        q_h(0, 0, 1)
+        il_v("v", 0, 0, 0, 256)
+        c_tensor(0, 2, 3)
+        turn_v(1, 7)
+        q_h(0, 0, 0)
+        q_v(0, 0, 0, 256)
+        q_h(0, 1, 0)
+        turn_h(1, 1, 0, 6)
+        turn_h(1, 1, 1, 5)
+        il_v("s", 1, 1, 256, 512)
+        q_h(0, 1, 1)
+        load_v(1, 0)
+        il_v("s", 1, 1, 0, 256)
+        load_h(1, 0)
+        c_diagonal(0, 1)
+        il_v("v", 0, 0, 256, 512)
+        c_tensor(0, 3, 3)
+        q_v(1, 1, 256, 512)
+        q_v(0, 0, 256, 512)
+        copy_h("s", 1, 1, 0)
+        c_vector(1, 2)
+        gains_product(0, 3, 6)
+        gains_product(0, 0, 4)
+        il_hul("v", 0, 768, 1024)
+        turn_h(1, 0, 1, 2)
+        il_hul("v", 0, 512, 768)
+        copy_h("s", 1, 1, 1)
+        il_v("s", 1, 0, 256, 512)
+        turn_h(1, 0, 0, 0)
+        il_v("v", 1, 0, 0, 256)
+        q_v(1, 0, 256, 512)
+        power(0, 3)
+        gains_product(0, 2, 5)
+        copy_h("s", 1, 0, 1)
+        q_h(1, 1, 1)
+        c_diagonal(0, 0)
+        gains_product(0, 1, 1)
+        c_tensor(1, 2, 2)
+        c_diagonal(0, 3)
+        power(0, 0)
+        q_v(1, 0, 0, 256)
+        load_hul(0, 0)
+        copy_h("s", 1, 0, 0)
+        q_h(1, 1, 0)
+        c_vector(1, 3)
+        c_vector(1, 1)
+        c_tensor(1, 1, 2)
+        load_hul(1, 0)
+        c_tensor(1, 3, 2)
+        load_hul(1, 1)
+        c_vector(1, 0)
+        q_h(1, 0, 0)
+        c_diagonal(0, 2)
+        power(0, 1)
+        power(0, 2)
+        q_hul(0, 1)
+        il_hul("s", 0, 256, 512)
+        il_hul("s", 0, 0, 256)
+        q_h(1, 0, 1)
+        weights_sum(0)
+        c_diagonal(1, 2)
+        gains_product(1, 2, 7)
+        weights_inverse(0)
+        c_diagonal(1, 1)
+        weights_gains(0)
+        q_v(1, 1, 0, 256)
+        scale_e(0, 2)
+        gains_product(1, 3, 0)
+        scale_e(0, 1)
+        power(1, 2)
+        gains_product(1, 0, 3)
+        power(1, 0)
+        scale_e(0, 0)
+        scale_e(0, 3)
+        power(1, 3)
+        q_hul(0, 0)
+        c_tensor(1, 0, 2)
+        q_e(0, 0)
+        gains_product(1, 1, 4)
+        q_e(0, 1)
+        c_diagonal(1, 3)
+        power(1, 1)
+        c_diagonal(1, 0)
+        back_product(0, 1, 0, 1)
+        back_product(0, 0, 0, 6)
+        subtract(0, 1, 0, 0, 4)
+        back_product(0, 0, 3, 1)
+        weights_sum(1)
+        back_product(0, 1, 1, 2)
+        il_hul("s", 1, 0, 256)
+        subtract(0, 0, 0, 0, 4)
+        back_product(0, 0, 2, 5)
+        weights_inverse(1)
+        back_product(0, 0, 1, 6)
+        subtract(0, 0, 3, 0, 4)
+        il_hul("s", 1, 512, 768)
+        weights_gains(1)
+        subtract(0, 1, 1, 0, 4)
+        il_hul("s", 1, 768, 1024)
+        subtract(0, 0, 1, 0, 4)
+        il_hul("s", 1, 256, 512)
+        subtract(0, 0, 2, 0, 4)
+        back_product(0, 1, 3, 1)
+        back_product(0, 1, 2, 6)
+        turn_d(0, 0, 3, 2)
+        scale_e(1, 0)
+        subtract(0, 1, 2, 0, 4)
+        subtract(0, 1, 3, 0, 4)
+        turn_d(0, 0, 2, 3)
+        copy_d("s", 0, 0, 3)
+        scale_e(1, 3)
+        turn_d(0, 0, 0, 5)
+        scale_e(1, 1)
+        copy_d("s", 0, 0, 2)
+        store_d(0, 0, 2, 4)
+        turn_d(0, 1, 0, 6)
+        turn_d(0, 1, 3, 2)
+        copy_d("s", 0, 0, 0)
+        scale_e(1, 2)
+        q_hul(1, 0)
+        q_e(1, 0)
+        turn_d(0, 1, 2, 0)
+        q_e(1, 1)
+        turn_d(0, 1, 1, 4)
+        copy_d("s", 0, 1, 2)
+        copy_d("s", 0, 1, 0)
+        turn_d(0, 0, 1, 5)
+        copy_d("s", 0, 1, 3)
+        copy_d("s", 0, 1, 1)
+        back_product(1, 0, 1, 7)
+        q_hul(1, 1)
+        copy_d("s", 0, 0, 1)
+        back_product(1, 0, 2, 6)
+        back_product(1, 0, 3, 1)
+        subtract(1, 0, 1, 0, 2)
+        subtract(1, 0, 1, 2, 4)
+        subtract(1, 0, 3, 2, 4)
+        il_d("s", 0, 1, 256, 512)
+        back_product(1, 0, 0, 2)
+        subtract(1, 0, 2, 0, 2)
+        back_product(1, 1, 0, 4)
+        il_d("s", 0, 1, 0, 256)
+        subtract(1, 0, 0, 0, 2)
+        subtract(1, 0, 2, 2, 4)
+        subtract(1, 0, 0, 2, 4)
+        back_product(1, 1, 2, 7)
+        subtract(1, 0, 3, 0, 2)
+        q_d(0, 1, 256, 512)
+        subtract(1, 1, 0, 2, 4)
+        back_product(1, 1, 3, 0)
+        subtract(1, 1, 2, 0, 2)
+        back_product(1, 1, 1, 5)
+        store_d(0, 1, 2, 4)
+        store_d(0, 0, 0, 2)
+        q_d(0, 1, 0, 256)
+        turn_d(1, 0, 3, 3)
+        il_d("v", 0, 0, 0, 256)
+        subtract(1, 1, 3, 0, 2)
+        turn_d(1, 0, 2, 1)
+        turn_d(1, 0, 1, 6)
+        subtract(1, 1, 1, 0, 2)
+        q_d(0, 0, 0, 256)
+        subtract(1, 1, 0, 0, 2)
+        turn_d(1, 0, 0, 2)
+        copy_d("s", 1, 0, 3)
+        copy_d("s", 1, 0, 2)
+        il_d("s", 0, 0, 256, 512)
+        store_d(0, 1, 0, 2)
+        store_codes(0, 1)
+        copy_d("s", 1, 0, 0)
+        turn_d(1, 1, 0, 3)
+        q_d(0, 0, 256, 512)
+        store_d(1, 0, 2, 4)
+        copy_d("s", 1, 0, 1)
+        subtract(1, 1, 2, 2, 4)
+        turn_d(1, 1, 1, 7)
+        store_codes(0, 0)
+        subtract(1, 1, 1, 2, 4)
+        subtract(1, 1, 3, 2, 4)
+        copy_d("s", 1, 1, 0)
+        il_d("v", 1, 0, 0, 256)
+        turn_d(1, 1, 3, 1)
+        il_d("v", 1, 0, 256, 512)
+        turn_d(1, 1, 2, 3)
+        copy_d("s", 1, 1, 1)
+        q_d(1, 0, 0, 256)
+        store_d(1, 0, 0, 2)
+        q_d(1, 0, 256, 512)
+        store_d(1, 1, 0, 2)
+        store_scales(0)
+        copy_d("s", 1, 1, 3)
+        store_codes(1, 0)
+        copy_d("s", 1, 1, 2)
+        il_d("s", 1, 1, 256, 512)
+        il_d("v", 1, 1, 0, 256)
+        q_d(1, 1, 0, 256)
+        q_d(1, 1, 256, 512)
+        store_d(1, 1, 2, 4)
+        store_codes(1, 1)
+        store_scales(1)

@@ -18,6 +18,7 @@ ACT = mybir.ActivationFunctionType
 P = 128
 G = N // 512
 LAST = 1
+SLOTS = 26
 C_ON_TENSOR = [(0, 0), (0, 1), (0, 2), (0, 3), (1, 0), (1, 1)]
 
 
@@ -47,16 +48,15 @@ def tile_wmmseunmatcheduplinkgradientsurrogate_kernel(tc, h, v, hul, u, a, s2, o
         w = per_f("w", [P, 4], F32)
         gains = per_f("gains", [P, 2, 4], F32)
         junk_v = sb.tile([P, 4, 256], F32, name="junk_v")
-        junk_s = sb.tile([P, 4, P], BF16, name="junk_s")
+        junk_s = sb.tile([P, 2, K], BF16, name="junk_s")
 
         h_sb = per_f("h_sb", [P, 4, N], BF16)
         v_sb = per_f("v_sb", [P, G, 4, K], BF16)
         hul_sb = per_f("hul_sb", [P, 4, N], BF16)
-        h_il = per_f("h_il", [P, G, K, 4], BF16)
-        v_il = per_f("v_il", [P, G, K, 4], BF16)
-        hul_il = per_f("hul_il", [P, N, 4], BF16)
-        e_il = per_f("e_il", [P, K, 4], BF16)
-        h_q, h_s = per_f("h_q", [P, G, K], U32), per_f("h_s", [P, G, K], U8)
+        h_il = per_f("h_il", [P, 2, G, 256, 4], BF16)
+        e_raw = per_f("e_raw", [P, 4, K], BF16)
+        stage = sb.tile([P, SLOTS * 256, 4], BF16, name="stage", align_bytes=64)
+        h_q, h_s = per_f("h_q", [P, 2, G, 256], U32), per_f("h_s", [P, 2, G, 256], U8)
         v_q, v_s = per_f("v_q", [P, G, K], U32), per_f("v_s", [P, G, K], U8)
         hul_q, hul_s = per_f("hul_q", [P, N], U32), per_f("hul_s", [P, N], U8)
         e_q, e_s = per_f("e_q", [P, K], U32), per_f("e_s", [P, K], U8)
@@ -67,15 +67,15 @@ def tile_wmmseunmatcheduplinkgradientsurrogate_kernel(tc, h, v, hul, u, a, s2, o
         def quantize(codes, scales, src):
             nc.vector.quantize_mx(out=codes.bitcast(FP8X4), scales=scales, in_=src.rearrange("p c t -> p (c t)"))
 
+        def slot(s, width):
+            return stage[:, 256 * s : 256 * s + width, :]
+
         def interleave(eng, dst, src):
-            dst4 = dst.rearrange("p (c i) t -> p c t i", i=4)
-            src4 = src.rearrange("p t (c i) -> p c t i", i=4)
-            if eng == "v":
-                nc.vector.tensor_copy(out=dst4, in_=src4)
-            elif eng == "s":
-                nc.scalar.copy(out=dst4, in_=src4)
+            if eng == "g":
+                nc.gpsimd.tensor_scalar(out=dst, in0=src.rearrange("p t c -> p c t"), scalar1=1.0, scalar2=0.0, op0=ALU.mult, op1=ALU.add)
             else:
-                nc.gpsimd.tensor_scalar(out=dst4, in0=src4, scalar1=1.0, scalar2=1.0, op0=ALU.mult, op1=ALU.mult)
+                copy = nc.vector.tensor_copy if eng == "v" else nc.scalar.copy
+                copy(out=dst.rearrange("p (c i) t -> p c t i", i=4), in_=src.rearrange("p t (c i) -> p c t i", i=4))
 
         def load_v(f, g):
             nc.sync.dma_start(out=v_sb[f][:, g], in_=v[f, 512 * g : 512 * (g + 1), :].rearrange("(p t) j -> p t j", t=4))
@@ -103,18 +103,17 @@ def tile_wmmseunmatcheduplinkgradientsurrogate_kernel(tc, h, v, hul, u, a, s2, o
             nc.vector.tensor_tensor(out=coef[:, :, 0, :], in0=a_bf[:], in1=usq[:], op=ALU.mult)
             nc.vector.tensor_tensor(out=terms[:, :, :, 0], in0=s2_bf[:], in1=usq[:], op=ALU.mult)
 
-        def il_v(eng, f, g, lo=0, hi=K):
-            interleave(eng, v_il[f][:, g, lo:hi, :], v_sb[f][:, g, :, lo:hi])
+        def il_v(eng, f, g, lo, hi, s):
+            interleave(eng, slot(s, hi - lo), v_sb[f][:, g, :, lo:hi])
 
-        def q_v(f, g, lo=0, hi=K):
-            quantize(v_q[f][:, g, lo:hi], v_s[f][:, g, lo:hi], v_il[f][:, g, lo:hi, :])
+        def q_v(f, g, lo, hi, s):
+            quantize(v_q[f][:, g, lo:hi], v_s[f][:, g, lo:hi], slot(s, hi - lo))
 
-        def il_hul(eng, f, lo, hi):
-            interleave(eng, hul_il[f][:, lo:hi, :], hul_sb[f][:, :, lo:hi])
+        def il_hul(eng, f, lo, hi, s):
+            interleave(eng, slot(s, hi - lo), hul_sb[f][:, :, lo:hi])
 
-        def q_hul(f, g):
-            cols = slice(512 * g, 512 * (g + 1))
-            quantize(hul_q[f][:, cols], hul_s[f][:, cols], hul_il[f][:, cols, :])
+        def q_hul(f, lo, hi, s):
+            quantize(hul_q[f][:, lo:hi], hul_s[f][:, lo:hi], slot(s, hi - lo))
 
         def turn_h(f, rp, g, b):
             acc = bank(b, f"ht{f}{rp}{g}")
@@ -126,14 +125,14 @@ def tile_wmmseunmatcheduplinkgradientsurrogate_kernel(tc, h, v, hul, u, a, s2, o
                     nc.tensor.transpose(acc[:, P * slot : P * (slot + 1)], words[:, 256 * g + half : 256 * (g + 1) : 2], ident[:])
 
         def copy_h(eng, f, rp, g):
-            dst = h_il[f][:, g, 256 * rp : 256 * (rp + 1), :].rearrange("p k t -> p (k t)").bitcast(F32)
+            dst = h_il[f][:, rp, g].rearrange("p k t -> p (k t)").bitcast(F32)
             copy = nc.vector.tensor_copy if eng == "v" else nc.scalar.copy
             copy(out=dst.rearrange("p (r m w) -> p r m w", r=2, w=2),
                  in_=live["ht", f, rp, g][:].rearrange("p (r w m) -> p r m w", r=2, w=2))
 
-        def q_h(f, rp, g):
-            cols = slice(256 * rp, 256 * (rp + 1))
-            quantize(h_q[f][:, g, cols], h_s[f][:, g, cols], h_il[f][:, g, cols, :])
+        def q_h(f, rp, lo, hi):
+            quantize(h_q[f][:, rp, lo:hi].rearrange("p g c -> p (g c)"), h_s[f][:, rp, lo:hi].rearrange("p g c -> p (g c)"),
+                     h_il[f][:, rp, lo:hi].rearrange("p g c t -> p (g c) t"))
 
         def turn_v(f, b):
             acc = bank(b, f"vt{f}")
@@ -157,7 +156,7 @@ def tile_wmmseunmatcheduplinkgradientsurrogate_kernel(tc, h, v, hul, u, a, s2, o
                 live["c", f] = bank(b, f"c{f}")
             acc = live["c", f]
             for n, (g, t) in enumerate(C_ON_TENSOR):
-                nc.tensor.matmul(acc[:, P * r : P * (r + 1)], lhsT=h_il[f][:, g, P * r : P * (r + 1), t],
+                nc.tensor.matmul(acc[:, P * r : P * (r + 1)], lhsT=h_il[f][:, r // 2, g, P * (r % 2) : P * (r % 2 + 1), t],
                                  rhs=v_sb[f][:, g, t, r::4], start=n == 0, stop=n == len(C_ON_TENSOR) - 1)
 
         def c_diagonal(f, r):
@@ -165,24 +164,21 @@ def tile_wmmseunmatcheduplinkgradientsurrogate_kernel(tc, h, v, hul, u, a, s2, o
                 out=junk_v[:, r, :P], in0=live["c", f][:, P * r : P * (r + 1)], scalar=m2u[:, f, r : r + 1],
                 in1=ident[:], op0=ALU.mult, op1=ALU.mult, accum_out=terms[:, f, r, 3:4])
 
-        def gains_product(f, jb, b):
-            acc = bank(b, f"p{f}{jb}")
-            live["p", f, jb] = acc
-            jc = slice(P * jb, P * (jb + 1))
-            for r in range(4):
-                kc = slice(P * r, P * (r + 1))
-                for g in range(G):
-                    nc.tensor.matmul_mx(out=acc[:, kc], lhsT=h_q[f][:, g, kc].bitcast(FP8X4), lhsT_scale=h_s[f][:, g, kc],
-                                        rhs=v_q[f][:, g, jc].bitcast(FP8X4), rhs_scale=v_s[f][:, g, jc],
-                                        start=g == 0, stop=g == G - 1)
+        def gains_product(f, r, b):
+            acc = bank(b, f"p{f}{r}")
+            live["p", f, r] = acc
+            kc = slice(P * (r % 2), P * (r % 2 + 1))
+            for g in range(G):
+                nc.tensor.matmul_mx(out=acc[:], lhsT=h_q[f][:, r // 2, g, kc].bitcast(FP8X4), lhsT_scale=h_s[f][:, r // 2, g, kc],
+                                    rhs=v_q[f][:, g, :].bitcast(FP8X4), rhs_scale=v_s[f][:, g, :],
+                                    start=g == 0, stop=g == G - 1)
 
-        def power(f, jb):
-            for r in range(4):
-                nc.scalar.activation(out=junk_s[:, r, :], in_=live["p", f, jb][:, P * r : P * (r + 1)], func=ACT.Square,
-                                     scale=u32[:, f, r : r + 1], accum_out=terms[:, f, r, 4 + jb : 5 + jb])
+        def power(f, r):
+            nc.scalar.activation(out=junk_s[:, r % 2, :], in_=live["p", f, r][:], func=ACT.Square,
+                                 scale=u32[:, f, r : r + 1], accum_out=terms[:, f, r, 4:5])
 
         def weights_sum(f):
-            nc.vector.tensor_reduce(out=mse[f][:], in_=terms[:, f], axis=mybir.AxisListType.X, op=ALU.add)
+            nc.vector.tensor_reduce(out=mse[f][:], in_=terms[:, f, :, :5], axis=mybir.AxisListType.X, op=ALU.add)
 
         def weights_inverse(f):
             nc.vector.reciprocal(out=w[f][:], in_=mse[f][:])
@@ -190,15 +186,20 @@ def tile_wmmseunmatcheduplinkgradientsurrogate_kernel(tc, h, v, hul, u, a, s2, o
         def weights_gains(f):
             nc.vector.tensor_tensor(out=gains[f][:], in0=coef[:, f], in1=w[f][:].unsqueeze(1).to_broadcast([P, 2, 4]), op=ALU.mult)
 
-        def scale_e(f, jb):
-            dst = e_il[f][:].rearrange("p (s b l) r -> p s b l r", s=4, b=4)[:, :, jb]
-            src = live["p", f, jb][:].rearrange("p (r l s) -> p s l r", r=4, s=4)
-            alpha = gains[f][:, 0, :].unsqueeze(1).unsqueeze(1).to_broadcast([P, 4, 32, 4])
-            nc.vector.tensor_tensor(out=dst, in0=src, in1=alpha, op=ALU.mult)
+        def scale_e(eng, f, r):
+            dst = e_raw[f][:, r, :].rearrange("p (s m) -> p s m", s=4)
+            src = live["p", f, r][:].rearrange("p (m s) -> p s m", s=4)
+            alpha = gains[f][:, 0, r : r + 1]
+            if eng == "v":
+                nc.vector.tensor_scalar(out=dst, in0=src, scalar1=alpha, scalar2=None, op0=ALU.mult)
+            else:
+                nc.scalar.activation(out=dst, in_=src, func=ACT.Copy, scale=alpha)
 
-        def q_e(f, half):
-            cols = slice(256 * half, 256 * (half + 1))
-            quantize(e_q[f][:, cols], e_s[f][:, cols], e_il[f][:, cols, :])
+        def il_e(eng, f, lo, hi, s):
+            interleave(eng, slot(s, hi - lo), e_raw[f][:, :, lo:hi])
+
+        def q_e(f, lo, hi, s):
+            quantize(e_q[f][:, lo:hi], e_s[f][:, lo:hi], slot(s, hi - lo))
 
         def back_product(f, g, r, b):
             acc = bank(b, f"d1{f}{g}{r}")
@@ -209,7 +210,7 @@ def tile_wmmseunmatcheduplinkgradientsurrogate_kernel(tc, h, v, hul, u, a, s2, o
 
         def subtract(f, g, r, lo, hi):
             if ("dt", f, g) not in live:
-                tag = f"dt{g}" if f == 0 else ("v_il0", "h_il0")[g]
+                tag = f"dt{g}" if f == 0 else f"h_il{g}"
                 live["dt", f, g] = sb.tile([P, 4, 512], F32, name=f"dt{f}{g}", tag=tag, align_bytes=64)
             nc.vector.scalar_tensor_tensor(
                 out=live["dt", f, g][:, r, :].rearrange("p (t i) -> p t i", t=4)[:, lo:hi],
@@ -237,13 +238,11 @@ def tile_wmmseunmatcheduplinkgradientsurrogate_kernel(tc, h, v, hul, u, a, s2, o
             rows = out_0[f, 512 * g : 512 * (g + 1), :].rearrange("(p t) j -> p t j", t=4)
             nc.sync.dma_start(out=rows[:, lo:hi, :], in_=live["dsb", f, g][:, lo:hi, :])
 
-        def il_d(eng, f, g, lo=0, hi=K):
-            if ("dil", f, g) not in live:
-                live["dil", f, g] = sb.tile([P, K, 4], BF16, name=f"dil{f}{g}", align_bytes=64)
-            interleave(eng, live["dil", f, g][:, lo:hi, :], live["dsb", f, g][:, :, lo:hi])
+        def il_d(eng, f, g, lo, hi, s):
+            interleave(eng, slot(s, hi - lo), live["dsb", f, g][:, :, lo:hi])
 
-        def q_d(f, g, lo=0, hi=K):
-            quantize(d_q[f][:, g, lo:hi], d_s[:, g, K * f + lo : K * f + hi], live["dil", f, g][:, lo:hi, :])
+        def q_d(f, g, lo, hi, s):
+            quantize(d_q[f][:, g, lo:hi], d_s[:, g, K * f + lo : K * f + hi], slot(s, hi - lo))
 
         def store_codes(f, g):
             words = out_1[g].rearrange("p m t -> p (m t)").bitcast(I32)
@@ -254,233 +253,227 @@ def tile_wmmseunmatcheduplinkgradientsurrogate_kernel(tc, h, v, hul, u, a, s2, o
             for q in range(4):
                 queues[q].dma_start(out=out_2[g, 4 * q : 4 * q + 4, :].bitcast(I32), in_=d_s[32 * q : 32 * q + 4, g, :].bitcast(I32))
 
-        load_vectors()
-        make_identity(nc, ident[:])
-        user_square()
         load_v(0, 1)
         load_h(0, 0)
-        turn_v(0, 4)
-        il_v("v", 0, 1, 0, 256)
-        turn_h(0, 0, 1, 3)
-        il_v("s", 0, 1, 256, 512)
-        user_terms()
-        q_v(0, 1, 0, 256)
-        copy_h("s", 0, 0, 1)
-        c_vector(0, 1)
-        c_vector(0, 0)
-        load_h(0, 1)
-        turn_h(0, 0, 0, 7)
-        copy_h("s", 0, 0, 0)
-        turn_h(0, 1, 0, 6)
         load_v(0, 0)
-        copy_h("s", 0, 1, 0)
-        turn_h(0, 1, 1, 1)
-        q_v(0, 1, 256, 512)
-        c_vector(0, 2)
+        load_h(0, 1)
+        make_identity(nc, ident[:])
+        load_vectors()
+        user_square()
+        user_terms()
+        il_v("v", 0, 1, 0, 256, 0)
+        turn_v(0, 2)
+        il_v("s", 0, 1, 256, 512, 1)
+        turn_h(0, 0, 0, 7)
+        turn_h(0, 0, 1, 0)
         load_v(1, 1)
-        load_h(1, 1)
-        load_hul(0, 1)
-        c_vector(0, 3)
-        c_tensor(0, 1, 3)
-        c_tensor(0, 0, 3)
-        copy_h("s", 0, 1, 1)
-        q_h(0, 0, 1)
-        il_v("v", 0, 0, 0, 256)
-        c_tensor(0, 2, 3)
-        turn_v(1, 7)
-        q_h(0, 0, 0)
-        q_v(0, 0, 0, 256)
-        q_h(0, 1, 0)
-        turn_h(1, 1, 0, 6)
-        turn_h(1, 1, 1, 5)
-        il_v("s", 1, 1, 256, 512)
-        q_h(0, 1, 1)
+        q_v(0, 1, 0, 512, 0)
+        turn_h(0, 1, 1, 4)
+        c_vector(0, 0)
+        il_v("s", 0, 0, 0, 256, 2)
+        il_v("v", 0, 0, 256, 512, 3)
         load_v(1, 0)
-        il_v("s", 1, 1, 0, 256)
-        load_h(1, 0)
-        c_diagonal(0, 1)
-        il_v("v", 0, 0, 256, 512)
-        c_tensor(0, 3, 3)
-        q_v(1, 1, 256, 512)
-        q_v(0, 0, 256, 512)
-        copy_h("s", 1, 1, 0)
-        c_vector(1, 2)
-        gains_product(0, 3, 6)
-        gains_product(0, 0, 4)
-        il_hul("v", 0, 768, 1024)
-        turn_h(1, 0, 1, 2)
-        il_hul("v", 0, 512, 768)
-        copy_h("s", 1, 1, 1)
-        il_v("s", 1, 0, 256, 512)
-        turn_h(1, 0, 0, 0)
-        il_v("v", 1, 0, 0, 256)
-        q_v(1, 0, 256, 512)
-        power(0, 3)
-        gains_product(0, 2, 5)
-        copy_h("s", 1, 0, 1)
-        q_h(1, 1, 1)
-        c_diagonal(0, 0)
-        gains_product(0, 1, 1)
-        c_tensor(1, 2, 2)
-        c_diagonal(0, 3)
-        power(0, 0)
-        q_v(1, 0, 0, 256)
+        copy_h("v", 0, 0, 1)
+        q_v(0, 0, 256, 512, 3)
+        copy_h("s", 0, 0, 0)
+        q_v(0, 0, 0, 256, 2)
+        q_h(0, 0, 0, 2)
+        c_vector(0, 1)
+        c_vector(0, 2)
+        il_v("s", 1, 1, 0, 256, 4)
         load_hul(0, 0)
-        copy_h("s", 1, 0, 0)
-        q_h(1, 1, 0)
-        c_vector(1, 3)
-        c_vector(1, 1)
-        c_tensor(1, 1, 2)
-        load_hul(1, 0)
-        c_tensor(1, 3, 2)
-        load_hul(1, 1)
-        c_vector(1, 0)
-        q_h(1, 0, 0)
-        c_diagonal(0, 2)
+        il_v("g", 1, 1, 256, 512, 2)
+        c_vector(0, 3)
+        copy_h("s", 0, 1, 1)
+        turn_h(0, 1, 0, 6)
+        gains_product(0, 1, 1)
+        c_tensor(0, 0, 3)
+        gains_product(0, 0, 0)
+        q_v(1, 1, 0, 256, 4)
+        q_v(1, 1, 256, 512, 2)
+        copy_h("s", 0, 1, 0)
         power(0, 1)
+        il_v("s", 1, 0, 0, 256, 6)
+        c_tensor(0, 1, 3)
+        q_h(0, 1, 0, 2)
+        il_v("v", 1, 0, 256, 512, 7)
+        load_hul(1, 0)
+        c_tensor(0, 2, 3)
+        load_h(1, 0)
+        il_hul("v", 0, 0, 512, 8)
+        c_tensor(0, 3, 3)
+        power(0, 0)
+        gains_product(0, 2, 4)
+        load_h(1, 1)
+        q_v(1, 0, 256, 512, 7)
+        gains_product(0, 3, 6)
+        turn_h(1, 0, 0, 5)
+        turn_h(1, 1, 0, 2)
+        il_hul("s", 1, 256, 512, 11)
+        q_v(1, 0, 0, 256, 6)
+        q_hul(0, 256, 512, 9)
         power(0, 2)
-        q_hul(0, 1)
-        il_hul("s", 0, 256, 512)
-        il_hul("s", 0, 0, 256)
-        q_h(1, 0, 1)
+        c_diagonal(0, 0)
+        load_hul(0, 1)
+        c_diagonal(0, 2)
+        turn_h(1, 0, 1, 7)
+        c_diagonal(0, 1)
+        il_hul("g", 1, 0, 256, 9)
+        power(0, 3)
+        copy_h("s", 1, 1, 0)
+        c_diagonal(0, 3)
+        copy_h("v", 1, 0, 0)
+        turn_v(1, 3)
+        turn_h(1, 1, 1, 2)
         weights_sum(0)
-        c_diagonal(1, 2)
-        gains_product(1, 2, 7)
+        copy_h("s", 1, 0, 1)
+        q_h(1, 0, 0, 1)
         weights_inverse(0)
-        c_diagonal(1, 1)
+        c_tensor(1, 1, 7)
+        q_hul(0, 0, 256, 8)
         weights_gains(0)
-        q_v(1, 1, 0, 256)
-        scale_e(0, 2)
-        gains_product(1, 3, 0)
-        scale_e(0, 1)
-        power(1, 2)
-        gains_product(1, 0, 3)
-        power(1, 0)
-        scale_e(0, 0)
-        scale_e(0, 3)
-        power(1, 3)
-        q_hul(0, 0)
-        c_tensor(1, 0, 2)
-        q_e(0, 0)
-        gains_product(1, 1, 4)
-        q_e(0, 1)
-        c_diagonal(1, 3)
-        power(1, 1)
+        scale_e("v", 0, 0)
+        c_vector(1, 0)
+        scale_e("s", 0, 1)
+        scale_e("s", 0, 3)
+        copy_h("v", 1, 1, 1)
+        c_tensor(1, 0, 7)
+        scale_e("s", 0, 2)
+        c_tensor(1, 2, 7)
+        il_hul("g", 0, 512, 768, 8)
+        q_hul(1, 0, 256, 9)
+        q_hul(1, 256, 512, 11)
+        q_h(1, 0, 1, 2)
+        il_e("s", 0, 0, 512, 12)
+        gains_product(1, 0, 2)
+        q_h(1, 1, 0, 2)
+        c_vector(1, 1)
         c_diagonal(1, 0)
-        back_product(0, 1, 0, 1)
-        back_product(0, 0, 0, 6)
-        subtract(0, 1, 0, 0, 4)
-        back_product(0, 0, 3, 1)
-        weights_sum(1)
-        back_product(0, 1, 1, 2)
-        il_hul("s", 1, 0, 256)
-        subtract(0, 0, 0, 0, 4)
-        back_product(0, 0, 2, 5)
-        weights_inverse(1)
-        back_product(0, 0, 1, 6)
+        c_vector(1, 2)
+        gains_product(1, 1, 6)
+        gains_product(1, 2, 0)
+        gains_product(1, 3, 1)
+        c_diagonal(1, 2)
+        c_diagonal(1, 1)
+        il_hul("g", 0, 768, 1024, 11)
+        c_tensor(1, 3, 7)
+        c_vector(1, 3)
+        q_e(0, 0, 512, 12)
+        q_hul(0, 768, 1024, 11)
+        power(1, 0)
+        power(1, 1)
+        back_product(0, 0, 3, 4)
+        q_hul(0, 512, 768, 8)
+        c_diagonal(1, 3)
+        back_product(0, 0, 0, 3)
+        power(1, 2)
         subtract(0, 0, 3, 0, 4)
-        il_hul("s", 1, 512, 768)
+        power(1, 3)
+        weights_sum(1)
+        weights_inverse(1)
+        back_product(0, 1, 1, 7)
         weights_gains(1)
-        subtract(0, 1, 1, 0, 4)
-        il_hul("s", 1, 768, 1024)
-        subtract(0, 0, 1, 0, 4)
-        il_hul("s", 1, 256, 512)
+        back_product(0, 0, 2, 5)
+        subtract(0, 0, 0, 0, 4)
         subtract(0, 0, 2, 0, 4)
-        back_product(0, 1, 3, 1)
-        back_product(0, 1, 2, 6)
-        turn_d(0, 0, 3, 2)
-        scale_e(1, 0)
-        subtract(0, 1, 2, 0, 4)
+        back_product(0, 0, 1, 4)
+        back_product(0, 1, 0, 3)
+        subtract(0, 0, 1, 0, 4)
+        scale_e("s", 1, 1)
+        back_product(0, 1, 3, 4)
+        scale_e("s", 1, 0)
+        back_product(0, 1, 2, 5)
+        scale_e("s", 1, 2)
+        subtract(0, 1, 1, 0, 4)
+        turn_d(0, 0, 3, 0)
+        scale_e("s", 1, 3)
+        load_hul(1, 1)
+        turn_d(0, 0, 1, 2)
+        il_hul("g", 1, 512, 768, 8)
+        subtract(0, 1, 0, 0, 4)
         subtract(0, 1, 3, 0, 4)
+        turn_d(0, 0, 0, 1)
         turn_d(0, 0, 2, 3)
+        subtract(0, 1, 2, 0, 4)
+        il_e("s", 1, 256, 512, 15)
+        turn_d(0, 1, 0, 7)
         copy_d("s", 0, 0, 3)
-        scale_e(1, 3)
-        turn_d(0, 0, 0, 5)
-        scale_e(1, 1)
+        turn_d(0, 1, 1, 5)
+        il_hul("g", 1, 768, 1024, 17)
+        q_e(1, 256, 512, 15)
+        back_product(1, 0, 3, 0)
         copy_d("s", 0, 0, 2)
-        store_d(0, 0, 2, 4)
-        turn_d(0, 1, 0, 6)
-        turn_d(0, 1, 3, 2)
+        il_e("v", 1, 0, 256, 14)
+        q_hul(1, 768, 1024, 17)
+        q_hul(1, 512, 768, 8)
+        back_product(1, 0, 2, 4)
+        q_e(1, 0, 256, 14)
+        subtract(1, 0, 2, 0, 4)
         copy_d("s", 0, 0, 0)
-        scale_e(1, 2)
-        q_hul(1, 0)
-        q_e(1, 0)
-        turn_d(0, 1, 2, 0)
-        q_e(1, 1)
-        turn_d(0, 1, 1, 4)
-        copy_d("s", 0, 1, 2)
-        copy_d("s", 0, 1, 0)
-        turn_d(0, 0, 1, 5)
-        copy_d("s", 0, 1, 3)
-        copy_d("s", 0, 1, 1)
-        back_product(1, 0, 1, 7)
-        q_hul(1, 1)
+        subtract(1, 0, 3, 0, 4)
+        turn_d(0, 1, 3, 6)
         copy_d("s", 0, 0, 1)
-        back_product(1, 0, 2, 6)
-        back_product(1, 0, 3, 1)
-        subtract(1, 0, 1, 0, 2)
-        subtract(1, 0, 1, 2, 4)
-        subtract(1, 0, 3, 2, 4)
-        il_d("s", 0, 1, 256, 512)
+        copy_d("s", 0, 1, 0)
+        copy_d("s", 0, 1, 1)
+        back_product(1, 0, 1, 3)
+        back_product(1, 1, 1, 1)
         back_product(1, 0, 0, 2)
-        subtract(1, 0, 2, 0, 2)
-        back_product(1, 1, 0, 4)
-        il_d("s", 0, 1, 0, 256)
-        subtract(1, 0, 0, 0, 2)
-        subtract(1, 0, 2, 2, 4)
-        subtract(1, 0, 0, 2, 4)
-        back_product(1, 1, 2, 7)
-        subtract(1, 0, 3, 0, 2)
-        q_d(0, 1, 256, 512)
-        subtract(1, 1, 0, 2, 4)
-        back_product(1, 1, 3, 0)
-        subtract(1, 1, 2, 0, 2)
-        back_product(1, 1, 1, 5)
-        store_d(0, 1, 2, 4)
-        store_d(0, 0, 0, 2)
-        q_d(0, 1, 0, 256)
-        turn_d(1, 0, 3, 3)
-        il_d("v", 0, 0, 0, 256)
-        subtract(1, 1, 3, 0, 2)
-        turn_d(1, 0, 2, 1)
-        turn_d(1, 0, 1, 6)
+        turn_d(0, 1, 2, 4)
+        back_product(1, 1, 0, 7)
+        copy_d("s", 0, 1, 3)
+        store_d(0, 0, 2, 4)
+        subtract(1, 0, 1, 0, 4)
+        subtract(1, 0, 0, 0, 4)
         subtract(1, 1, 1, 0, 2)
-        q_d(0, 0, 0, 256)
+        back_product(1, 1, 3, 6)
         subtract(1, 1, 0, 0, 2)
-        turn_d(1, 0, 0, 2)
-        copy_d("s", 1, 0, 3)
-        copy_d("s", 1, 0, 2)
-        il_d("s", 0, 0, 256, 512)
-        store_d(0, 1, 0, 2)
-        store_codes(0, 1)
-        copy_d("s", 1, 0, 0)
-        turn_d(1, 1, 0, 3)
-        q_d(0, 0, 256, 512)
-        store_d(1, 0, 2, 4)
+        il_d("g", 0, 0, 256, 512, 14)
+        il_d("g", 0, 0, 0, 256, 18)
+        copy_d("s", 0, 1, 2)
+        subtract(1, 1, 3, 0, 2)
+        q_d(0, 0, 256, 512, 14)
+        turn_d(1, 0, 1, 3)
+        q_d(0, 0, 0, 256, 18)
         copy_d("s", 1, 0, 1)
-        subtract(1, 1, 2, 2, 4)
-        turn_d(1, 1, 1, 7)
-        store_codes(0, 0)
-        subtract(1, 1, 1, 2, 4)
+        turn_d(1, 0, 0, 4)
+        il_d("g", 0, 1, 256, 512, 18)
+        store_d(0, 0, 0, 2)
+        subtract(1, 1, 0, 2, 4)
+        copy_d("s", 1, 0, 0)
+        turn_d(1, 0, 2, 2)
+        back_product(1, 1, 2, 5)
+        turn_d(1, 0, 3, 0)
+        subtract(1, 1, 2, 0, 2)
         subtract(1, 1, 3, 2, 4)
-        copy_d("s", 1, 1, 0)
-        il_d("v", 1, 0, 0, 256)
-        turn_d(1, 1, 3, 1)
-        il_d("v", 1, 0, 256, 512)
-        turn_d(1, 1, 2, 3)
-        copy_d("s", 1, 1, 1)
-        q_d(1, 0, 0, 256)
+        subtract(1, 1, 2, 2, 4)
+        copy_d("s", 1, 0, 2)
+        copy_d("s", 1, 0, 3)
+        store_d(0, 1, 0, 2)
+        subtract(1, 1, 1, 2, 4)
+        store_d(0, 1, 2, 4)
+        store_codes(0, 0)
+        turn_d(1, 1, 0, 4)
         store_d(1, 0, 0, 2)
-        q_d(1, 0, 256, 512)
+        turn_d(1, 1, 1, 7)
+        copy_d("s", 1, 1, 0)
+        il_d("v", 1, 0, 0, 512, 20)
+        store_d(1, 0, 2, 4)
+        turn_d(1, 1, 3, 0)
+        turn_d(1, 1, 2, 2)
+        copy_d("s", 1, 1, 1)
         store_d(1, 1, 0, 2)
+        q_d(1, 0, 0, 512, 20)
         store_scales(0)
+        il_d("v", 0, 1, 0, 256, 22)
         copy_d("s", 1, 1, 3)
         store_codes(1, 0)
         copy_d("s", 1, 1, 2)
-        il_d("s", 1, 1, 256, 512)
-        il_d("v", 1, 1, 0, 256)
-        q_d(1, 1, 0, 256)
-        q_d(1, 1, 256, 512)
+        il_d("v", 1, 1, 256, 512, 25)
+        q_d(0, 1, 256, 512, 18)
+        q_d(0, 1, 0, 256, 22)
+        il_d("s", 1, 1, 0, 256, 24)
+        q_d(1, 1, 0, 512, 24)
         store_d(1, 1, 2, 4)
-        store_codes(1, 1)
+        store_codes(0, 1)
         store_scales(1)
+        store_codes(1, 1)

@@ -17,7 +17,6 @@ ACT = mybir.ActivationFunctionType
 
 P = 128
 G = N // 512
-LAST = 1
 SLOTS = 26
 C_ON_TENSOR = [(0, 0), (0, 1), (0, 2), (0, 3), (1, 0), (1, 1)]
 
@@ -248,232 +247,230 @@ def tile_wmmseunmatcheduplinkgradientsurrogate_kernel(tc, h, v, hul, u, a, s2, o
             words = out_1[g].rearrange("p m t -> p (m t)").bitcast(I32)
             nc.sync.dma_start(out=words[:, K * f : K * (f + 1)], in_=d_q[f][:, g, :].bitcast(I32))
 
-        def store_scales(g):
-            queues = (nc.sync, nc.scalar, nc.sync, nc.scalar) if g == LAST else (nc.sync,) * 4
+        def store_scales(lo, hi):
+            queues = (nc.sync, nc.scalar, nc.sync, nc.scalar)
             for q in range(4):
-                queues[q].dma_start(out=out_2[g, 4 * q : 4 * q + 4, :].bitcast(I32), in_=d_s[32 * q : 32 * q + 4, g, :].bitcast(I32))
+                rows = out_2[lo:hi, 4 * q : 4 * q + 4, :].rearrange("g r m -> r g m")
+                queues[q].dma_start(out=rows.bitcast(I32), in_=d_s[32 * q : 32 * q + 4, lo:hi, :].bitcast(I32))
 
-        load_v(0, 1)
-        load_h(0, 0)
-        load_v(0, 0)
-        load_h(0, 1)
         make_identity(nc, ident[:])
+        load_v(0, 1)
         load_vectors()
+        turn_v(0, 2)
+        load_h(0, 0)
         user_square()
         user_terms()
         il_v("v", 0, 1, 0, 256, 0)
-        turn_v(0, 2)
+        load_h(0, 1)
         il_v("s", 0, 1, 256, 512, 1)
+        q_v(0, 1, 0, 256, 0)
+        load_v(0, 0)
+        turn_h(0, 0, 1, 4)
         turn_h(0, 0, 0, 7)
-        turn_h(0, 0, 1, 0)
-        load_v(1, 1)
-        q_v(0, 1, 0, 512, 0)
-        turn_h(0, 1, 1, 4)
-        c_vector(0, 0)
-        il_v("s", 0, 0, 0, 256, 2)
-        il_v("v", 0, 0, 256, 512, 3)
-        load_v(1, 0)
-        copy_h("v", 0, 0, 1)
-        q_v(0, 0, 256, 512, 3)
-        copy_h("s", 0, 0, 0)
-        q_v(0, 0, 0, 256, 2)
-        q_h(0, 0, 0, 2)
+        copy_h("s", 0, 0, 1)
         c_vector(0, 1)
+        copy_h("s", 0, 0, 0)
+        turn_h(0, 1, 0, 1)
+        q_v(0, 1, 256, 512, 1)
+        c_vector(0, 0)
         c_vector(0, 2)
-        il_v("s", 1, 1, 0, 256, 4)
-        load_hul(0, 0)
-        il_v("g", 1, 1, 256, 512, 2)
-        c_vector(0, 3)
-        copy_h("s", 0, 1, 1)
-        turn_h(0, 1, 0, 6)
-        gains_product(0, 1, 1)
-        c_tensor(0, 0, 3)
-        gains_product(0, 0, 0)
-        q_v(1, 1, 0, 256, 4)
-        q_v(1, 1, 256, 512, 2)
         copy_h("s", 0, 1, 0)
-        power(0, 1)
-        il_v("s", 1, 0, 0, 256, 6)
-        c_tensor(0, 1, 3)
+        load_v(1, 1)
+        load_hul(0, 0)
+        turn_h(0, 1, 1, 4)
+        q_h(0, 0, 0, 2)
+        copy_h("s", 0, 1, 1)
+        c_tensor(0, 1, 0)
+        il_v("v", 0, 0, 0, 512, 4)
+        c_tensor(0, 0, 0)
+        c_tensor(0, 3, 0)
         q_h(0, 1, 0, 2)
-        il_v("v", 1, 0, 256, 512, 7)
-        load_hul(1, 0)
-        c_tensor(0, 2, 3)
+        q_v(0, 0, 256, 512, 5)
+        c_tensor(0, 2, 0)
         load_h(1, 0)
-        il_hul("v", 0, 0, 512, 8)
-        c_tensor(0, 3, 3)
-        power(0, 0)
-        gains_product(0, 2, 4)
-        load_h(1, 1)
-        q_v(1, 0, 256, 512, 7)
-        gains_product(0, 3, 6)
-        turn_h(1, 0, 0, 5)
-        turn_h(1, 1, 0, 2)
-        il_hul("s", 1, 256, 512, 11)
-        q_v(1, 0, 0, 256, 6)
-        q_hul(0, 256, 512, 9)
-        power(0, 2)
-        c_diagonal(0, 0)
-        load_hul(0, 1)
-        c_diagonal(0, 2)
-        turn_h(1, 0, 1, 7)
+        q_v(0, 0, 0, 256, 4)
+        il_hul("v", 0, 0, 256, 6)
         c_diagonal(0, 1)
-        il_hul("g", 1, 0, 256, 9)
-        power(0, 3)
-        copy_h("s", 1, 1, 0)
         c_diagonal(0, 3)
-        copy_h("v", 1, 0, 0)
-        turn_v(1, 3)
-        turn_h(1, 1, 1, 2)
+        c_diagonal(0, 0)
+        c_diagonal(0, 2)
+        c_vector(0, 3)
+        il_v("s", 1, 1, 0, 512, 2)
+        gains_product(0, 1, 1)
+        gains_product(0, 3, 4)
+        gains_product(0, 0, 5)
+        power(0, 1)
+        power(0, 3)
+        gains_product(0, 2, 0)
+        il_hul("g", 0, 256, 512, 4)
+        load_v(1, 0)
+        power(0, 0)
+        power(0, 2)
+        load_h(1, 1)
+        turn_h(1, 0, 1, 7)
+        q_v(1, 1, 0, 512, 2)
+        turn_h(1, 0, 0, 3)
+        il_v("v", 1, 0, 0, 512, 8)
+        turn_h(1, 1, 1, 6)
         weights_sum(0)
+        q_v(1, 0, 0, 512, 8)
         copy_h("s", 1, 0, 1)
-        q_h(1, 0, 0, 1)
         weights_inverse(0)
-        c_tensor(1, 1, 7)
-        q_hul(0, 0, 256, 8)
-        weights_gains(0)
-        scale_e("v", 0, 0)
-        c_vector(1, 0)
-        scale_e("s", 0, 1)
-        scale_e("s", 0, 3)
-        copy_h("v", 1, 1, 1)
-        c_tensor(1, 0, 7)
-        scale_e("s", 0, 2)
-        c_tensor(1, 2, 7)
-        il_hul("g", 0, 512, 768, 8)
-        q_hul(1, 0, 256, 9)
-        q_hul(1, 256, 512, 11)
-        q_h(1, 0, 1, 2)
-        il_e("s", 0, 0, 512, 12)
-        gains_product(1, 0, 2)
-        q_h(1, 1, 0, 2)
-        c_vector(1, 1)
-        c_diagonal(1, 0)
-        c_vector(1, 2)
-        gains_product(1, 1, 6)
-        gains_product(1, 2, 0)
-        gains_product(1, 3, 1)
-        c_diagonal(1, 2)
-        c_diagonal(1, 1)
-        il_hul("g", 0, 768, 1024, 11)
-        c_tensor(1, 3, 7)
-        c_vector(1, 3)
-        q_e(0, 0, 512, 12)
-        q_hul(0, 768, 1024, 11)
-        power(1, 0)
-        power(1, 1)
-        back_product(0, 0, 3, 4)
-        q_hul(0, 512, 768, 8)
-        c_diagonal(1, 3)
-        back_product(0, 0, 0, 3)
-        power(1, 2)
-        subtract(0, 0, 3, 0, 4)
-        power(1, 3)
-        weights_sum(1)
-        weights_inverse(1)
-        back_product(0, 1, 1, 7)
-        weights_gains(1)
-        back_product(0, 0, 2, 5)
-        subtract(0, 0, 0, 0, 4)
-        subtract(0, 0, 2, 0, 4)
-        back_product(0, 0, 1, 4)
-        back_product(0, 1, 0, 3)
-        subtract(0, 0, 1, 0, 4)
-        scale_e("s", 1, 1)
-        back_product(0, 1, 3, 4)
-        scale_e("s", 1, 0)
-        back_product(0, 1, 2, 5)
-        scale_e("s", 1, 2)
-        subtract(0, 1, 1, 0, 4)
-        turn_d(0, 0, 3, 0)
-        scale_e("s", 1, 3)
         load_hul(1, 1)
+        copy_h("s", 1, 0, 0)
+        q_h(1, 0, 1, 2)
+        turn_v(1, 7)
+        weights_gains(0)
+        copy_h("s", 1, 1, 1)
+        q_h(1, 0, 0, 1)
+        turn_h(1, 1, 0, 2)
+        scale_e("s", 0, 2)
+        q_hul(0, 256, 512, 4)
+        q_hul(0, 0, 256, 6)
+        scale_e("v", 0, 1)
+        load_hul(0, 1)
+        c_tensor(1, 1, 3)
+        scale_e("s", 0, 3)
+        c_vector(1, 2)
+        scale_e("s", 0, 0)
+        c_vector(1, 3)
+        c_tensor(1, 0, 3)
+        copy_h("s", 1, 1, 0)
+        c_vector(1, 0)
+        c_vector(1, 1)
+        il_e("s", 0, 0, 256, 10)
+        gains_product(1, 0, 0)
+        gains_product(1, 1, 6)
+        q_h(1, 1, 0, 2)
+        power(1, 1)
+        il_hul("g", 0, 512, 768, 6)
+        il_e("v", 0, 256, 512, 11)
+        q_e(0, 0, 256, 10)
+        c_tensor(1, 2, 3)
+        gains_product(1, 2, 1)
+        load_hul(1, 0)
+        q_e(0, 256, 512, 11)
+        c_diagonal(1, 0)
+        back_product(0, 0, 1, 7)
+        c_diagonal(1, 1)
+        back_product(0, 0, 2, 5)
+        subtract(0, 0, 1, 0, 4)
+        il_hul("g", 0, 768, 1024, 11)
+        back_product(0, 0, 0, 2)
+        il_hul("g", 1, 256, 512, 13)
+        power(1, 0)
+        il_hul("s", 1, 768, 1024, 15)
+        gains_product(1, 3, 4)
+        subtract(0, 0, 2, 0, 4)
+        back_product(0, 0, 3, 7)
+        c_tensor(1, 3, 3)
+        power(1, 2)
+        subtract(0, 0, 0, 0, 4)
+        power(1, 3)
+        subtract(0, 0, 3, 0, 4)
+        il_hul("s", 1, 512, 768, 14)
         turn_d(0, 0, 1, 2)
-        il_hul("g", 1, 512, 768, 8)
-        subtract(0, 1, 0, 0, 4)
-        subtract(0, 1, 3, 0, 4)
-        turn_d(0, 0, 0, 1)
-        turn_d(0, 0, 2, 3)
-        subtract(0, 1, 2, 0, 4)
-        il_e("s", 1, 256, 512, 15)
-        turn_d(0, 1, 0, 7)
-        copy_d("s", 0, 0, 3)
-        turn_d(0, 1, 1, 5)
-        il_hul("g", 1, 768, 1024, 17)
-        q_e(1, 256, 512, 15)
-        back_product(1, 0, 3, 0)
-        copy_d("s", 0, 0, 2)
-        il_e("v", 1, 0, 256, 14)
-        q_hul(1, 768, 1024, 17)
-        q_hul(1, 512, 768, 8)
-        back_product(1, 0, 2, 4)
-        q_e(1, 0, 256, 14)
-        subtract(1, 0, 2, 0, 4)
-        copy_d("s", 0, 0, 0)
-        subtract(1, 0, 3, 0, 4)
-        turn_d(0, 1, 3, 6)
+        c_diagonal(1, 2)
+        c_diagonal(1, 3)
+        q_hul(0, 768, 1024, 11)
+        q_hul(0, 512, 768, 6)
+        weights_sum(1)
+        turn_d(0, 0, 0, 7)
+        q_hul(1, 512, 768, 14)
+        weights_inverse(1)
+        q_hul(1, 256, 512, 13)
         copy_d("s", 0, 0, 1)
+        back_product(0, 1, 3, 5)
+        copy_d("s", 0, 0, 0)
+        back_product(0, 1, 0, 3)
+        weights_gains(1)
+        back_product(0, 1, 1, 2)
+        subtract(0, 1, 3, 0, 4)
+        back_product(0, 1, 2, 7)
+        subtract(0, 1, 1, 0, 4)
+        scale_e("s", 1, 1)
+        scale_e("s", 1, 0)
+        subtract(0, 1, 2, 0, 4)
+        il_hul("g", 1, 0, 256, 13)
+        scale_e("s", 1, 2)
+        subtract(0, 1, 0, 0, 4)
+        turn_d(0, 0, 3, 5)
+        turn_d(0, 0, 2, 7)
+        scale_e("s", 1, 3)
+        store_d(0, 0, 0, 2)
+        turn_d(0, 1, 0, 3)
+        copy_d("s", 0, 0, 3)
         copy_d("s", 0, 1, 0)
+        q_hul(1, 0, 256, 13)
+        turn_d(0, 1, 3, 1)
+        copy_d("s", 0, 1, 3)
+        il_e("v", 1, 0, 512, 16)
+        copy_d("s", 0, 0, 2)
+        il_d("g", 0, 0, 256, 512, 13)
+        turn_d(0, 1, 1, 2)
+        turn_d(0, 1, 2, 4)
+        q_e(1, 0, 512, 16)
         copy_d("s", 0, 1, 1)
         back_product(1, 0, 1, 3)
-        back_product(1, 1, 1, 1)
-        back_product(1, 0, 0, 2)
-        turn_d(0, 1, 2, 4)
-        back_product(1, 1, 0, 7)
-        copy_d("s", 0, 1, 3)
-        store_d(0, 0, 2, 4)
-        subtract(1, 0, 1, 0, 4)
-        subtract(1, 0, 0, 0, 4)
-        subtract(1, 1, 1, 0, 2)
-        back_product(1, 1, 3, 6)
-        subtract(1, 1, 0, 0, 2)
-        il_d("g", 0, 0, 256, 512, 14)
-        il_d("g", 0, 0, 0, 256, 18)
+        q_hul(1, 768, 1024, 15)
+        back_product(1, 0, 3, 6)
         copy_d("s", 0, 1, 2)
-        subtract(1, 1, 3, 0, 2)
-        q_d(0, 0, 256, 512, 14)
-        turn_d(1, 0, 1, 3)
-        q_d(0, 0, 0, 256, 18)
-        copy_d("s", 1, 0, 1)
-        turn_d(1, 0, 0, 4)
-        il_d("g", 0, 1, 256, 512, 18)
-        store_d(0, 0, 0, 2)
-        subtract(1, 1, 0, 2, 4)
-        copy_d("s", 1, 0, 0)
-        turn_d(1, 0, 2, 2)
-        back_product(1, 1, 2, 5)
-        turn_d(1, 0, 3, 0)
-        subtract(1, 1, 2, 0, 2)
-        subtract(1, 1, 3, 2, 4)
-        subtract(1, 1, 2, 2, 4)
-        copy_d("s", 1, 0, 2)
-        copy_d("s", 1, 0, 3)
+        store_d(0, 0, 2, 4)
         store_d(0, 1, 0, 2)
-        subtract(1, 1, 1, 2, 4)
+        back_product(1, 0, 2, 0)
+        subtract(1, 0, 1, 0, 4)
+        back_product(1, 0, 0, 5)
+        subtract(1, 0, 2, 0, 4)
+        il_d("g", 0, 1, 0, 256, 15)
+        back_product(1, 1, 3, 7)
+        il_d("s", 0, 0, 0, 256, 18)
+        subtract(1, 0, 3, 0, 4)
+        subtract(1, 0, 0, 0, 4)
+        back_product(1, 1, 0, 2)
+        back_product(1, 1, 1, 1)
+        subtract(1, 1, 1, 0, 2)
+        q_d(0, 0, 0, 256, 18)
+        back_product(1, 1, 2, 4)
+        q_d(0, 0, 256, 512, 13)
+        q_d(0, 1, 0, 256, 15)
+        il_d("s", 0, 1, 256, 512, 21)
+        turn_d(1, 0, 1, 0)
+        q_d(0, 1, 256, 512, 21)
+        turn_d(1, 0, 0, 6)
+        subtract(1, 1, 3, 0, 2)
+        turn_d(1, 0, 3, 5)
+        turn_d(1, 0, 2, 3)
         store_d(0, 1, 2, 4)
+        copy_d("s", 1, 0, 1)
+        copy_d("s", 1, 0, 0)
         store_codes(0, 0)
-        turn_d(1, 1, 0, 4)
-        store_d(1, 0, 0, 2)
-        turn_d(1, 1, 1, 7)
-        copy_d("s", 1, 1, 0)
-        il_d("v", 1, 0, 0, 512, 20)
-        store_d(1, 0, 2, 4)
-        turn_d(1, 1, 3, 0)
-        turn_d(1, 1, 2, 2)
-        copy_d("s", 1, 1, 1)
-        store_d(1, 1, 0, 2)
-        q_d(1, 0, 0, 512, 20)
-        store_scales(0)
-        il_d("v", 0, 1, 0, 256, 22)
-        copy_d("s", 1, 1, 3)
-        store_codes(1, 0)
-        copy_d("s", 1, 1, 2)
-        il_d("v", 1, 1, 256, 512, 25)
-        q_d(0, 1, 256, 512, 18)
-        q_d(0, 1, 0, 256, 22)
-        il_d("s", 1, 1, 0, 256, 24)
-        q_d(1, 1, 0, 512, 24)
-        store_d(1, 1, 2, 4)
+        subtract(1, 1, 2, 0, 2)
         store_codes(0, 1)
-        store_scales(1)
+        subtract(1, 1, 0, 0, 2)
+        copy_d("s", 1, 0, 3)
+        copy_d("s", 1, 0, 2)
+        subtract(1, 1, 1, 2, 4)
+        turn_d(1, 1, 1, 6)
+        store_d(1, 0, 0, 2)
+        subtract(1, 1, 0, 2, 4)
+        subtract(1, 1, 2, 2, 4)
+        subtract(1, 1, 3, 2, 4)
+        copy_d("s", 1, 1, 1)
+        turn_d(1, 1, 0, 3)
+        turn_d(1, 1, 2, 4)
+        il_d("v", 1, 0, 0, 512, 22)
+        copy_d("s", 1, 1, 0)
+        copy_d("s", 1, 1, 2)
+        turn_d(1, 1, 3, 0)
+        store_d(1, 0, 2, 4)
+        q_d(1, 0, 0, 512, 22)
+        copy_d("s", 1, 1, 3)
+        il_d("v", 1, 1, 0, 256, 24)
+        q_d(1, 1, 0, 256, 24)
+        store_d(1, 1, 0, 2)
+        store_codes(1, 0)
+        store_d(1, 1, 2, 4)
+        il_d("s", 1, 1, 256, 512, 25)
+        q_d(1, 1, 256, 512, 25)
         store_codes(1, 1)
+        store_scales(0, 2)

@@ -16,13 +16,18 @@ ALU = mybir.AluOpType
 ACT = mybir.ActivationFunctionType
 
 P = 128
-G = N // 512
-SLOTS = 26
+PASS = 512
+G = N // PASS
+HALF = PASS // 2
+SLOTS = range(4)
 C_ON_TENSOR = [(0, 0), (0, 1), (0, 2), (0, 3), (1, 0), (1, 1)]
+STAGE_COLUMNS = 13 * PASS
+NOISE, ONE, C_VECTOR, C_TENSOR, POWER, N_TERMS = 0, 1, 2, 3, 4, 5
 
 
 def tile_wmmseunmatcheduplinkgradientsurrogate_kernel(tc, h, v, hul, u, a, s2, out_0, out_1, out_2):
     nc = tc.nc
+    vector, scalar, gpsimd = nc.vector, nc.scalar, nc.gpsimd
     with ExitStack() as ctx:
         sb = ctx.enter_context(tc.tile_pool(name="sb", bufs=1))
         ps = ctx.enter_context(tc.psum_pool(name="ps", bufs=1))
@@ -31,446 +36,427 @@ def tile_wmmseunmatcheduplinkgradientsurrogate_kernel(tc, h, v, hul, u, a, s2, o
         def per_f(name, shape, dtype):
             return [sb.tile(shape, dtype, name=f"{name}{f}", align_bytes=64) for f in range(F)]
 
-        def bank(b, name):
-            return ps.tile([P, 512], F32, name=name, tag=f"bank{b}")
-
         ident = sb.tile([P, P], F32, name="ident")
-        u_bf = sb.tile([P, F, 4], BF16, name="u_bf")
-        a_bf = sb.tile([P, F, 4], BF16, name="a_bf")
-        s2_bf = sb.tile([P, F, 4], BF16, name="s2_bf")
-        u32 = sb.tile([P, F, 4], F32, name="u32")
+        rows = sb.tile([P, K], BF16, name="rows")
+        vec = sb.tile([P, 3, F, 4], F32, name="vec")
         usq = sb.tile([P, F, 4], F32, name="usq")
         m2u = sb.tile([P, F, 4], F32, name="m2u")
         coef = sb.tile([P, F, 2, 4], F32, name="coef")
         terms = sb.tile([P, F, 4, 8], F32, name="terms")
         mse = per_f("mse", [P, 4], F32)
-        w = per_f("w", [P, 4], F32)
+        weight = per_f("weight", [P, 4], F32)
         gains = per_f("gains", [P, 2, 4], F32)
-        junk_v = sb.tile([P, 4, 256], F32, name="junk_v")
+        junk_v = sb.tile([P, 4, HALF], F32, name="junk_v")
         junk_s = sb.tile([P, 2, K], BF16, name="junk_s")
 
         h_sb = per_f("h_sb", [P, 4, N], BF16)
         v_sb = per_f("v_sb", [P, G, 4, K], BF16)
-        hul_sb = per_f("hul_sb", [P, 4, N], BF16)
-        h_il = per_f("h_il", [P, 2, G, 256, 4], BF16)
+        hul_sb = per_f("hul_sb", [P, G, 4, PASS], BF16)
+        h_il = per_f("h_il", [P, 2, G, HALF, 4], BF16)
         e_raw = per_f("e_raw", [P, 4, K], BF16)
-        stage = sb.tile([P, SLOTS * 256, 4], BF16, name="stage", align_bytes=64)
-        h_q, h_s = per_f("h_q", [P, 2, G, 256], U32), per_f("h_s", [P, 2, G, 256], U8)
+        stage = sb.tile([P, STAGE_COLUMNS, 4], BF16, name="stage", align_bytes=64)
+        h_q, h_s = per_f("h_q", [P, 2, G, HALF], U32), per_f("h_s", [P, 2, G, HALF], U8)
         v_q, v_s = per_f("v_q", [P, G, K], U32), per_f("v_s", [P, G, K], U8)
         hul_q, hul_s = per_f("hul_q", [P, N], U32), per_f("hul_s", [P, N], U8)
         e_q, e_s = per_f("e_q", [P, K], U32), per_f("e_s", [P, K], U8)
         d_q = per_f("d_q", [P, G, K], U32)
         d_s = sb.tile([P, G, F * K], U8, name="d_s", align_bytes=64)
+
         live = {}
+        home = {}
+        staged = {}
+        last_read = [0]
+
+        def bank(b, *key):
+            live[key] = ps.tile([P, PASS], F32, name="_".join(map(str, key)), tag=f"bank{b}")
+            return live[key]
+
+        def block(n):
+            return slice(P * n, P * (n + 1))
+
+        def copy(eng, out, in_):
+            if eng is vector:
+                vector.tensor_copy(out=out, in_=in_)
+            else:
+                scalar.copy(out=out, in_=in_)
 
         def quantize(codes, scales, src):
-            nc.vector.quantize_mx(out=codes.bitcast(FP8X4), scales=scales, in_=src.rearrange("p c t -> p (c t)"))
+            vector.quantize_mx(out=codes.bitcast(FP8X4), scales=scales, in_=src.rearrange("p c t -> p (c t)"))
 
-        def slot(s, width):
-            return stage[:, 256 * s : 256 * s + width, :]
-
-        def interleave(eng, dst, src):
-            if eng == "g":
-                nc.gpsimd.tensor_scalar(out=dst, in0=src.rearrange("p t c -> p c t"), scalar1=1.0, scalar2=0.0, op0=ALU.mult, op1=ALU.add)
+        def interleave(eng, operand, src, lo, hi, reuse):
+            if reuse:
+                first = last_read[0]
             else:
-                copy = nc.vector.tensor_copy if eng == "v" else nc.scalar.copy
-                copy(out=dst.rearrange("p (c i) t -> p c t i", i=4), in_=src.rearrange("p t (c i) -> p c t i", i=4))
+                first = home.setdefault(operand, PASS * len(home)) + lo
+            for col in range(lo, hi, HALF):
+                staged[operand, col] = first + col - lo
+            dst, src = stage[:, first : first + hi - lo, :], src[:, :, lo:hi]
+            if eng is gpsimd:
+                gpsimd.tensor_scalar(out=dst, in0=src.rearrange("p t c -> p c t"), scalar1=1.0, scalar2=0.0,
+                                     op0=ALU.mult, op1=ALU.add)
+            else:
+                copy(eng, dst.rearrange("p (c x) t -> p c t x", x=4), src.rearrange("p t (c x) -> p c t x", x=4))
+
+        def quantize_staged(operand, codes, scales, lo, hi):
+            first = staged[operand, lo]
+            last_read[0] = first
+            quantize(codes[:, lo:hi], scales[:, lo:hi], stage[:, first : first + hi - lo, :])
 
         def load_v(f, g):
-            nc.sync.dma_start(out=v_sb[f][:, g], in_=v[f, 512 * g : 512 * (g + 1), :].rearrange("(p t) j -> p t j", t=4))
+            nc.sync.dma_start(out=v_sb[f][:, g], in_=v[f, PASS * g : PASS * (g + 1), :].rearrange("(i t) j -> i t j", t=4))
 
-        def load_h(f, rp):
-            rows = h[f].rearrange("(p r) n -> p r n", r=4)
-            nc.sync.dma_start(out=h_sb[f][:, 2 * rp : 2 * rp + 2, :], in_=rows[:, 2 * rp : 2 * rp + 2, :])
+        def load_h(f, pair):
+            users = slice(2 * pair, 2 * pair + 2)
+            nc.sync.dma_start(out=h_sb[f][:, users, :], in_=h[f].rearrange("(m r) n -> m r n", r=4)[:, users, :])
 
         def load_hul(f, g):
-            cols = slice(512 * g, 512 * (g + 1))
-            nc.sync.dma_start(out=hul_sb[f][:, :, cols], in_=hul[f].rearrange("(p r) n -> p r n", r=4)[:, :, cols])
+            antennas = slice(PASS * g, PASS * (g + 1))
+            nc.sync.dma_start(out=hul_sb[f][:, g], in_=hul[f].rearrange("(m r) n -> m r n", r=4)[:, :, antennas])
 
         def load_vectors():
-            for dst, src in ((u_bf, u), (a_bf, a), (s2_bf, s2)):
-                nc.scalar.dma_start(out=dst[:], in_=src.rearrange("f (p r) -> p f r", r=4))
+            gpsimd.memset(rows[:].bitcast(F32), 0.0)
+            for n, src in enumerate((u, a, s2)):
+                nc.sync.dma_start(out=rows[F * n : F * (n + 1), :], in_=src)
 
-        def user_square():
-            nc.scalar.activation(out=usq[:], in_=u_bf[:], func=ACT.Square)
+        def turn_vectors(b):
+            acc = bank(b, "vectors")
+            words = rows[:].bitcast(F32)
+            for x in range(2):
+                nc.tensor.transpose(acc[:, block(x)], words[:, x::2], ident[:])
+
+        def unpack_vectors():
+            turned = live["vectors",][:, : 2 * P].bitcast(BF16).rearrange("p (x row y) -> p row x y", x=2, y=2)
+            scalar.activation(out=usq[:].rearrange("p f (x y) -> p f x y", x=2), in_=turned[:, :F], func=ACT.Square)
+            scalar.copy(out=vec[:].rearrange("p n f (x y) -> p (n f) x y", x=2), in_=turned[:, : 3 * F])
 
         def user_terms():
-            nc.vector.memset(terms[:, :, :, 1], 1.0)
-            nc.vector.tensor_copy(out=u32[:], in_=u_bf[:])
-            nc.vector.tensor_scalar(out=m2u[:], in0=u_bf[:], scalar1=-2.0, scalar2=None, op0=ALU.mult)
-            nc.vector.scalar_tensor_tensor(out=coef[:, :, 1, :], in0=a_bf[:], scalar=-1.0, in1=u_bf[:], op0=ALU.mult, op1=ALU.mult)
-            nc.vector.tensor_tensor(out=coef[:, :, 0, :], in0=a_bf[:], in1=usq[:], op=ALU.mult)
-            nc.vector.tensor_tensor(out=terms[:, :, :, 0], in0=s2_bf[:], in1=usq[:], op=ALU.mult)
+            vector.memset(terms[:, :, :, ONE], 1.0)
+            vector.tensor_scalar(out=m2u[:], in0=vec[:, 0], scalar1=-2.0, scalar2=None, op0=ALU.mult)
+            vector.scalar_tensor_tensor(out=coef[:, :, 1, :], in0=vec[:, 1], scalar=-1.0, in1=vec[:, 0],
+                                        op0=ALU.mult, op1=ALU.mult)
+            vector.tensor_tensor(out=coef[:, :, 0, :], in0=vec[:, 1], in1=usq[:], op=ALU.mult)
+            vector.tensor_tensor(out=terms[:, :, :, NOISE], in0=vec[:, 2], in1=usq[:], op=ALU.mult)
 
-        def il_v(eng, f, g, lo, hi, s):
-            interleave(eng, slot(s, hi - lo), v_sb[f][:, g, :, lo:hi])
+        def il_v(eng, f, g, lo=0, hi=PASS, reuse=False):
+            interleave(eng, ("v", f, g), v_sb[f][:, g], lo, hi, reuse)
 
-        def q_v(f, g, lo, hi, s):
-            quantize(v_q[f][:, g, lo:hi], v_s[f][:, g, lo:hi], slot(s, hi - lo))
+        def q_v(f, g, lo=0, hi=PASS):
+            quantize_staged(("v", f, g), v_q[f][:, g, :], v_s[f][:, g, :], lo, hi)
 
-        def il_hul(eng, f, lo, hi, s):
-            interleave(eng, slot(s, hi - lo), hul_sb[f][:, :, lo:hi])
-
-        def q_hul(f, lo, hi, s):
-            quantize(hul_q[f][:, lo:hi], hul_s[f][:, lo:hi], slot(s, hi - lo))
-
-        def turn_h(f, rp, g, b):
-            acc = bank(b, f"ht{f}{rp}{g}")
-            live["ht", f, rp, g] = acc
+        def turn_h(f, pair, g, b):
+            acc = bank(b, "hT", f, pair, g)
             for rr in range(2):
-                words = h_sb[f][:, 2 * rp + rr, :].bitcast(F32)
-                for half in range(2):
-                    slot = 2 * rr + half
-                    nc.tensor.transpose(acc[:, P * slot : P * (slot + 1)], words[:, 256 * g + half : 256 * (g + 1) : 2], ident[:])
+                words = h_sb[f][:, 2 * pair + rr, :].bitcast(F32)
+                for x in range(2):
+                    nc.tensor.transpose(acc[:, block(2 * rr + x)], words[:, HALF * g + x : HALF * (g + 1) : 2], ident[:])
 
-        def copy_h(eng, f, rp, g):
-            dst = h_il[f][:, rp, g].rearrange("p k t -> p (k t)").bitcast(F32)
-            copy = nc.vector.tensor_copy if eng == "v" else nc.scalar.copy
-            copy(out=dst.rearrange("p (r m w) -> p r m w", r=2, w=2),
-                 in_=live["ht", f, rp, g][:].rearrange("p (r w m) -> p r m w", r=2, w=2))
+        def copy_h(f, pair, g):
+            words = h_il[f][:, pair, g].rearrange("p k t -> p (k t)").bitcast(F32)
+            scalar.copy(out=words.rearrange("p (r m x) -> p r m x", r=2, x=2),
+                        in_=live["hT", f, pair, g][:].rearrange("p (r x m) -> p r m x", r=2, x=2))
 
-        def q_h(f, rp, lo, hi):
-            quantize(h_q[f][:, rp, lo:hi].rearrange("p g c -> p (g c)"), h_s[f][:, rp, lo:hi].rearrange("p g c -> p (g c)"),
-                     h_il[f][:, rp, lo:hi].rearrange("p g c t -> p (g c) t"))
+        def q_h(f, pair, g_lo=0, g_hi=G):
+            quantize(h_q[f][:, pair, g_lo:g_hi].rearrange("p g c -> p (g c)"),
+                     h_s[f][:, pair, g_lo:g_hi].rearrange("p g c -> p (g c)"),
+                     h_il[f][:, pair, g_lo:g_hi].rearrange("p g c t -> p (g c) t"))
 
         def turn_v(f, b):
-            acc = bank(b, f"vt{f}")
-            live["vt", f] = acc
+            acc = bank(b, "vT", f)
             for tt in range(2):
                 words = v_sb[f][:, 1, 2 + tt, :].bitcast(F32)
-                for half in range(2):
-                    slot = 2 * tt + half
-                    nc.tensor.transpose(acc[:, P * slot : P * (slot + 1)], words[:, half::2], ident[:])
+                for x in range(2):
+                    nc.tensor.transpose(acc[:, block(2 * tt + x)], words[:, x::2], ident[:])
 
         def c_vector(f, r):
-            vt = live["vt", f][:].bitcast(BF16).rearrange("p (t w i e) -> p t w i e", t=2, w=2, e=2)
-            hr = h_sb[f][:, r, 512:].rearrange("p (i t) -> p t i", t=4)
-            nc.vector.scalar_tensor_tensor(
-                out=junk_v[:, r, :].rearrange("p (t i) -> p t i", t=2), in0=vt[:, :, r // 2, :, r % 2],
-                scalar=m2u[:, f, r : r + 1], in1=hr[:, 2:4, :], op0=ALU.mult, op1=ALU.mult,
-                accum_out=terms[:, f, r, 2:3])
+            v_turned = live["vT", f][:].bitcast(BF16).rearrange("p (t x i y) -> p t x i y", t=2, x=2, y=2)
+            h_row = h_sb[f][:, r, PASS:].rearrange("p (i t) -> p t i", t=4)
+            vector.scalar_tensor_tensor(
+                out=junk_v[:, r, :].rearrange("p (t i) -> p t i", t=2), in0=v_turned[:, :, r // 2, :, r % 2],
+                scalar=m2u[:, f, r : r + 1], in1=h_row[:, 2:4, :], op0=ALU.mult, op1=ALU.mult,
+                accum_out=terms[:, f, r, C_VECTOR : C_VECTOR + 1])
 
         def c_tensor(f, r, b):
-            if ("c", f) not in live:
-                live["c", f] = bank(b, f"c{f}")
-            acc = live["c", f]
+            acc = bank(b, "c", f) if r == 0 else live["c", f]
             for n, (g, t) in enumerate(C_ON_TENSOR):
-                nc.tensor.matmul(acc[:, P * r : P * (r + 1)], lhsT=h_il[f][:, r // 2, g, P * (r % 2) : P * (r % 2 + 1), t],
+                nc.tensor.matmul(acc[:, block(r)], lhsT=h_il[f][:, r // 2, g, block(r % 2), t],
                                  rhs=v_sb[f][:, g, t, r::4], start=n == 0, stop=n == len(C_ON_TENSOR) - 1)
 
         def c_diagonal(f, r):
-            nc.vector.scalar_tensor_tensor(
-                out=junk_v[:, r, :P], in0=live["c", f][:, P * r : P * (r + 1)], scalar=m2u[:, f, r : r + 1],
-                in1=ident[:], op0=ALU.mult, op1=ALU.mult, accum_out=terms[:, f, r, 3:4])
+            vector.scalar_tensor_tensor(
+                out=junk_v[:, r, :P], in0=live["c", f][:, block(r)], scalar=m2u[:, f, r : r + 1], in1=ident[:],
+                op0=ALU.mult, op1=ALU.mult, accum_out=terms[:, f, r, C_TENSOR : C_TENSOR + 1])
 
-        def gains_product(f, r, b):
-            acc = bank(b, f"p{f}{r}")
-            live["p", f, r] = acc
-            kc = slice(P * (r % 2), P * (r % 2 + 1))
+        def first_product(f, r, b):
+            acc = bank(b, "p", f, r)
             for g in range(G):
-                nc.tensor.matmul_mx(out=acc[:], lhsT=h_q[f][:, r // 2, g, kc].bitcast(FP8X4), lhsT_scale=h_s[f][:, r // 2, g, kc],
+                nc.tensor.matmul_mx(out=acc[:], lhsT=h_q[f][:, r // 2, g, block(r % 2)].bitcast(FP8X4),
+                                    lhsT_scale=h_s[f][:, r // 2, g, block(r % 2)],
                                     rhs=v_q[f][:, g, :].bitcast(FP8X4), rhs_scale=v_s[f][:, g, :],
                                     start=g == 0, stop=g == G - 1)
 
         def power(f, r):
-            nc.scalar.activation(out=junk_s[:, r % 2, :], in_=live["p", f, r][:], func=ACT.Square,
-                                 scale=u32[:, f, r : r + 1], accum_out=terms[:, f, r, 4:5])
+            scalar.activation(out=junk_s[:, r % 2, :], in_=live["p", f, r][:], func=ACT.Square,
+                              scale=vec[:, 0, f, r : r + 1], accum_out=terms[:, f, r, POWER : POWER + 1])
 
         def weights_sum(f):
-            nc.vector.tensor_reduce(out=mse[f][:], in_=terms[:, f, :, :5], axis=mybir.AxisListType.X, op=ALU.add)
+            vector.tensor_reduce(out=mse[f][:], in_=terms[:, f, :, :N_TERMS], axis=mybir.AxisListType.X, op=ALU.add)
 
         def weights_inverse(f):
-            nc.vector.reciprocal(out=w[f][:], in_=mse[f][:])
+            vector.reciprocal(out=weight[f][:], in_=mse[f][:])
 
         def weights_gains(f):
-            nc.vector.tensor_tensor(out=gains[f][:], in0=coef[:, f], in1=w[f][:].unsqueeze(1).to_broadcast([P, 2, 4]), op=ALU.mult)
+            vector.tensor_tensor(out=gains[f][:], in0=coef[:, f], in1=weight[f][:].unsqueeze(1).to_broadcast([P, 2, 4]),
+                                 op=ALU.mult)
 
-        def scale_e(eng, f, r):
-            dst = e_raw[f][:, r, :].rearrange("p (s m) -> p s m", s=4)
-            src = live["p", f, r][:].rearrange("p (m s) -> p s m", s=4)
-            alpha = gains[f][:, 0, r : r + 1]
-            if eng == "v":
-                nc.vector.tensor_scalar(out=dst, in0=src, scalar1=alpha, scalar2=None, op0=ALU.mult)
-            else:
-                nc.scalar.activation(out=dst, in_=src, func=ACT.Copy, scale=alpha)
+        def scale_e(f, r):
+            scalar.activation(out=e_raw[f][:, r, :].rearrange("p (s m) -> p s m", s=4),
+                              in_=live["p", f, r][:].rearrange("p (m s) -> p s m", s=4),
+                              func=ACT.Copy, scale=gains[f][:, 0, r : r + 1])
 
-        def il_e(eng, f, lo, hi, s):
-            interleave(eng, slot(s, hi - lo), e_raw[f][:, :, lo:hi])
+        def il_e(eng, f, lo=0, hi=PASS):
+            interleave(eng, ("e", f), e_raw[f][:], lo, hi, False)
 
-        def q_e(f, lo, hi, s):
-            quantize(e_q[f][:, lo:hi], e_s[f][:, lo:hi], slot(s, hi - lo))
+        def q_e(f, lo, hi):
+            quantize_staged(("e", f), e_q[f][:], e_s[f][:], lo, hi)
 
-        def back_product(f, g, r, b):
-            acc = bank(b, f"d1{f}{g}{r}")
-            live["d1", f, g, r] = acc
-            jc, nc_ = slice(P * r, P * (r + 1)), slice(512 * g, 512 * (g + 1))
-            nc.tensor.matmul_mx(out=acc[:], lhsT=e_q[f][:, jc].bitcast(FP8X4), lhsT_scale=e_s[f][:, jc],
-                                rhs=hul_q[f][:, nc_].bitcast(FP8X4), rhs_scale=hul_s[f][:, nc_], start=True, stop=True)
+        def il_hul(eng, f, g, lo=0, hi=PASS, reuse=False):
+            interleave(eng, ("hul", f, g), hul_sb[f][:, g], lo, hi, reuse)
 
-        def subtract(f, g, r, lo, hi):
-            if ("dt", f, g) not in live:
-                tag = f"dt{g}" if f == 0 else f"h_il{g}"
-                live["dt", f, g] = sb.tile([P, 4, 512], F32, name=f"dt{f}{g}", tag=tag, align_bytes=64)
-            nc.vector.scalar_tensor_tensor(
-                out=live["dt", f, g][:, r, :].rearrange("p (t i) -> p t i", t=4)[:, lo:hi],
-                in0=hul_sb[f][:, r, 512 * g : 512 * (g + 1)].rearrange("p (i t) -> p t i", t=4)[:, lo:hi],
-                scalar=gains[f][:, 1, r : r + 1], in1=live["d1", f, g, r][:].rearrange("p (i t) -> p t i", t=4)[:, lo:hi],
+        def q_hul(f, g, lo, hi):
+            antennas = slice(PASS * g, PASS * (g + 1))
+            quantize_staged(("hul", f, g), hul_q[f][:, antennas], hul_s[f][:, antennas], lo, hi)
+
+        def second_product(f, g, r, b):
+            acc = bank(b, "d1T", f, g, r)
+            antennas = slice(PASS * g, PASS * (g + 1))
+            nc.tensor.matmul_mx(out=acc[:], lhsT=e_q[f][:, block(r)].bitcast(FP8X4), lhsT_scale=e_s[f][:, block(r)],
+                                rhs=hul_q[f][:, antennas].bitcast(FP8X4), rhs_scale=hul_s[f][:, antennas],
+                                start=True, stop=True)
+
+        def subtract(f, g, r, t_lo=0, t_hi=4):
+            if ("dT", f, g) not in live:
+                tag = f"dT{g}" if f == 0 else f"h_il{g}"
+                live["dT", f, g] = sb.tile([P, 4, PASS], F32, name=f"dT{f}{g}", tag=tag, align_bytes=64)
+            vector.scalar_tensor_tensor(
+                out=live["dT", f, g][:, r, :].rearrange("p (t i) -> p t i", t=4)[:, t_lo:t_hi],
+                in0=hul_sb[f][:, g, r, :].rearrange("p (i t) -> p t i", t=4)[:, t_lo:t_hi],
+                scalar=gains[f][:, 1, r : r + 1],
+                in1=live["d1T", f, g, r][:].rearrange("p (i t) -> p t i", t=4)[:, t_lo:t_hi],
                 op0=ALU.mult, op1=ALU.add)
 
         def turn_d(f, g, t, b):
-            acc = bank(b, f"d{f}{g}{t}")
-            live["d", f, g, t] = acc
-            for r in range(4):
-                nc.tensor.transpose(acc[:, P * r : P * (r + 1)], live["dt", f, g][:, r, P * t : P * (t + 1)], ident[:])
+            acc = bank(b, "d", f, g, t)
+            for r in SLOTS:
+                nc.tensor.transpose(acc[:, block(r)], live["dT", f, g][:, r, block(t)], ident[:])
 
         def copy_d(eng, f, g, t):
-            if ("dsb", f, g) not in live:
-                live["dsb", f, g] = sb.tile([P, 4, K], F32, name=f"dsb{f}{g}")
-            dst = live["dsb", f, g][:, t, :].rearrange("p (m r) -> p m r", r=4)
-            src = live["d", f, g, t][:].rearrange("p (r m) -> p m r", r=4)
-            if eng == "v":
-                nc.vector.tensor_copy(out=dst, in_=src)
-            else:
-                nc.scalar.copy(out=dst, in_=src)
+            if ("d_sb", f, g) not in live:
+                live["d_sb", f, g] = sb.tile([P, 4, K], F32, name=f"d_sb{f}{g}")
+            copy(eng, live["d_sb", f, g][:, t, :].rearrange("p (m r) -> p m r", r=4),
+                 live["d", f, g, t][:].rearrange("p (r m) -> p m r", r=4))
 
-        def store_d(f, g, lo, hi):
-            rows = out_0[f, 512 * g : 512 * (g + 1), :].rearrange("(p t) j -> p t j", t=4)
-            nc.sync.dma_start(out=rows[:, lo:hi, :], in_=live["dsb", f, g][:, lo:hi, :])
+        def store_d(f, g, pair):
+            slots = slice(2 * pair, 2 * pair + 2)
+            dst = out_0[f, PASS * g : PASS * (g + 1), :].rearrange("(i t) j -> i t j", t=4)
+            nc.sync.dma_start(out=dst[:, slots, :], in_=live["d_sb", f, g][:, slots, :])
 
-        def il_d(eng, f, g, lo, hi, s):
-            interleave(eng, slot(s, hi - lo), live["dsb", f, g][:, :, lo:hi])
+        def il_d(eng, f, g, lo=0, hi=PASS, reuse=False):
+            interleave(eng, ("d", f, g), live["d_sb", f, g][:], lo, hi, reuse)
 
-        def q_d(f, g, lo, hi, s):
-            quantize(d_q[f][:, g, lo:hi], d_s[:, g, K * f + lo : K * f + hi], slot(s, hi - lo))
+        def q_d(f, g, lo=0, hi=PASS):
+            quantize_staged(("d", f, g), d_q[f][:, g, :], d_s[:, g, K * f : K * (f + 1)], lo, hi)
 
         def store_codes(f, g):
             words = out_1[g].rearrange("p m t -> p (m t)").bitcast(I32)
             nc.sync.dma_start(out=words[:, K * f : K * (f + 1)], in_=d_q[f][:, g, :].bitcast(I32))
 
-        def store_scales(lo, hi):
-            queues = (nc.sync, nc.scalar, nc.sync, nc.scalar)
-            for q in range(4):
-                rows = out_2[lo:hi, 4 * q : 4 * q + 4, :].rearrange("g r m -> r g m")
-                queues[q].dma_start(out=rows.bitcast(I32), in_=d_s[32 * q : 32 * q + 4, lo:hi, :].bitcast(I32))
+        def store_scales():
+            for q, queue in enumerate((nc.sync, scalar, nc.sync, scalar)):
+                dst = out_2[:, 4 * q : 4 * q + 4, :].rearrange("g row m -> row g m")
+                queue.dma_start(out=dst.bitcast(I32), in_=d_s[32 * q : 32 * q + 4].bitcast(I32))
 
-        make_identity(nc, ident[:])
+        LOW, HIGH = (0, HALF), (HALF, PASS)
+
         load_v(0, 1)
         load_vectors()
-        turn_v(0, 2)
         load_h(0, 0)
-        user_square()
-        user_terms()
-        il_v("v", 0, 1, 0, 256, 0)
         load_h(0, 1)
-        il_v("s", 0, 1, 256, 512, 1)
-        q_v(0, 1, 0, 256, 0)
         load_v(0, 0)
-        turn_h(0, 0, 1, 4)
-        turn_h(0, 0, 0, 7)
-        copy_h("s", 0, 0, 1)
-        c_vector(0, 1)
-        copy_h("s", 0, 0, 0)
-        turn_h(0, 1, 0, 1)
-        q_v(0, 1, 256, 512, 1)
-        c_vector(0, 0)
-        c_vector(0, 2)
-        copy_h("s", 0, 1, 0)
         load_v(1, 1)
         load_hul(0, 0)
-        turn_h(0, 1, 1, 4)
-        q_h(0, 0, 0, 2)
-        copy_h("s", 0, 1, 1)
-        c_tensor(0, 1, 0)
-        il_v("v", 0, 0, 0, 512, 4)
-        c_tensor(0, 0, 0)
-        c_tensor(0, 3, 0)
-        q_h(0, 1, 0, 2)
-        q_v(0, 0, 256, 512, 5)
-        c_tensor(0, 2, 0)
-        load_h(1, 0)
-        q_v(0, 0, 0, 256, 4)
-        il_hul("v", 0, 0, 256, 6)
-        c_diagonal(0, 1)
-        c_diagonal(0, 3)
-        c_diagonal(0, 0)
-        c_diagonal(0, 2)
-        c_vector(0, 3)
-        il_v("s", 1, 1, 0, 512, 2)
-        gains_product(0, 1, 1)
-        gains_product(0, 3, 4)
-        gains_product(0, 0, 5)
-        power(0, 1)
-        power(0, 3)
-        gains_product(0, 2, 0)
-        il_hul("g", 0, 256, 512, 4)
         load_v(1, 0)
-        power(0, 0)
-        power(0, 2)
+        load_h(1, 0)
         load_h(1, 1)
-        turn_h(1, 0, 1, 7)
-        q_v(1, 1, 0, 512, 2)
-        turn_h(1, 0, 0, 3)
-        il_v("v", 1, 0, 0, 512, 8)
-        turn_h(1, 1, 1, 6)
-        weights_sum(0)
-        q_v(1, 0, 0, 512, 8)
-        copy_h("s", 1, 0, 1)
-        weights_inverse(0)
-        load_hul(1, 1)
-        copy_h("s", 1, 0, 0)
-        q_h(1, 0, 1, 2)
-        turn_v(1, 7)
-        weights_gains(0)
-        copy_h("s", 1, 1, 1)
-        q_h(1, 0, 0, 1)
-        turn_h(1, 1, 0, 2)
-        scale_e("s", 0, 2)
-        q_hul(0, 256, 512, 4)
-        q_hul(0, 0, 256, 6)
-        scale_e("v", 0, 1)
         load_hul(0, 1)
-        c_tensor(1, 1, 3)
-        scale_e("s", 0, 3)
-        c_vector(1, 2)
-        scale_e("s", 0, 0)
-        c_vector(1, 3)
-        c_tensor(1, 0, 3)
-        copy_h("s", 1, 1, 0)
-        c_vector(1, 0)
-        c_vector(1, 1)
-        il_e("s", 0, 0, 256, 10)
-        gains_product(1, 0, 0)
-        gains_product(1, 1, 6)
-        q_h(1, 1, 0, 2)
-        power(1, 1)
-        il_hul("g", 0, 512, 768, 6)
-        il_e("v", 0, 256, 512, 11)
-        q_e(0, 0, 256, 10)
-        c_tensor(1, 2, 3)
-        gains_product(1, 2, 1)
         load_hul(1, 0)
-        q_e(0, 256, 512, 11)
-        c_diagonal(1, 0)
-        back_product(0, 0, 1, 7)
-        c_diagonal(1, 1)
-        back_product(0, 0, 2, 5)
-        subtract(0, 0, 1, 0, 4)
-        il_hul("g", 0, 768, 1024, 11)
-        back_product(0, 0, 0, 2)
-        il_hul("g", 1, 256, 512, 13)
+        load_hul(1, 1)
+        make_identity(nc, ident[:])
+
+        turn_vectors(7)
+        unpack_vectors()
+        turn_v(0, 6)
+        il_v(vector, 0, 1, *LOW)
+        il_v(scalar, 0, 1, *HIGH)
+        user_terms()
+        q_v(0, 1, *LOW)
+        c_vector(0, 0)
+        c_vector(0, 1)
+        q_v(0, 1, *HIGH)
+        c_vector(0, 2)
+        for pair in range(2):
+            for g in range(G):
+                turn_h(0, pair, g, 2 * pair + g)
+                copy_h(0, pair, g)
+        q_h(0, 0)
+        il_v(vector, 0, 0)
+        q_h(0, 1)
+        q_v(0, 0)
+        for r in SLOTS:
+            c_tensor(0, r, 4)
+        il_v(scalar, 1, 1)
+        for r in SLOTS:
+            first_product(0, r, r)
+            power(0, r)
+        il_hul(vector, 0, 0)
+        q_hul(0, 0, *LOW)
+        il_v(gpsimd, 1, 0, *LOW, reuse=True)
+        c_vector(0, 3)
+        for r in SLOTS:
+            c_diagonal(0, r)
+        q_hul(0, 0, *HIGH)
+        il_v(vector, 1, 0, *HIGH)
+
+        for pair, g, b in ((0, 0, 5), (0, 1, 7), (1, 0, 4)):
+            turn_h(1, pair, g, b)
+            copy_h(1, pair, g)
+        turn_h(1, 1, 1, 6)
+        turn_v(1, 5)
+        weights_sum(0)
+        q_v(1, 1, *LOW)
+        weights_inverse(0)
+        q_v(1, 1, *HIGH)
+        weights_gains(0)
+        q_h(1, 0)
+        q_v(1, 0, *LOW)
+        q_v(1, 0, *HIGH)
+        il_hul(gpsimd, 0, 1, *LOW, reuse=True)
+        for r in SLOTS:
+            scale_e(0, r)
+        copy_h(1, 1, 1)
+        c_tensor(1, 0, 7)
+        first_product(1, 0, 4)
+        first_product(1, 1, 0)
+        c_tensor(1, 1, 7)
+        c_tensor(1, 2, 7)
+        for r in SLOTS:
+            c_vector(1, r)
+        q_h(1, 1, 0, 1)
+        il_e(vector, 0, *LOW)
+        il_e(scalar, 0, *HIGH)
+        q_h(1, 1, 1, 2)
+        q_e(0, *LOW)
+        q_e(0, *HIGH)
+        il_hul(gpsimd, 1, 0, *LOW, reuse=True)
+
+        second_product(0, 0, 0, 1)
+        second_product(0, 0, 1, 2)
+        first_product(1, 2, 3)
+        first_product(1, 3, 6)
+        second_product(0, 0, 2, 5)
         power(1, 0)
-        il_hul("s", 1, 768, 1024, 15)
-        gains_product(1, 3, 4)
-        subtract(0, 0, 2, 0, 4)
-        back_product(0, 0, 3, 7)
-        c_tensor(1, 3, 3)
-        power(1, 2)
-        subtract(0, 0, 0, 0, 4)
-        power(1, 3)
-        subtract(0, 0, 3, 0, 4)
-        il_hul("s", 1, 512, 768, 14)
-        turn_d(0, 0, 1, 2)
-        c_diagonal(1, 2)
+        il_hul(scalar, 0, 1, *HIGH)
+        for r in (1, 2, 3):
+            power(1, r)
+        il_hul(scalar, 1, 0, *HIGH)
+        for r in (0, 1, 2):
+            c_diagonal(1, r)
+        c_tensor(1, 3, 7)
+        subtract(0, 0, 0)
+        second_product(0, 0, 3, 1)
+        subtract(0, 0, 1)
+        q_hul(0, 1, *LOW)
+        q_hul(0, 1, *HIGH)
+        il_hul(gpsimd, 1, 1, *LOW, reuse=True)
+        second_product(0, 1, 0, 2)
+        subtract(0, 0, 2)
+        second_product(0, 1, 1, 5)
         c_diagonal(1, 3)
-        q_hul(0, 768, 1024, 11)
-        q_hul(0, 512, 768, 6)
+        second_product(0, 1, 2, 7)
+        subtract(0, 0, 3)
+        turn_d(0, 0, 0, 1)
         weights_sum(1)
-        turn_d(0, 0, 0, 7)
-        q_hul(1, 512, 768, 14)
+        subtract(0, 1, 0)
+        second_product(0, 1, 3, 2)
         weights_inverse(1)
-        q_hul(1, 256, 512, 13)
-        copy_d("s", 0, 0, 1)
-        back_product(0, 1, 3, 5)
-        copy_d("s", 0, 0, 0)
-        back_product(0, 1, 0, 3)
         weights_gains(1)
-        back_product(0, 1, 1, 2)
-        subtract(0, 1, 3, 0, 4)
-        back_product(0, 1, 2, 7)
-        subtract(0, 1, 1, 0, 4)
-        scale_e("s", 1, 1)
-        scale_e("s", 1, 0)
-        subtract(0, 1, 2, 0, 4)
-        il_hul("g", 1, 0, 256, 13)
-        scale_e("s", 1, 2)
-        subtract(0, 1, 0, 0, 4)
-        turn_d(0, 0, 3, 5)
-        turn_d(0, 0, 2, 7)
-        scale_e("s", 1, 3)
-        store_d(0, 0, 0, 2)
-        turn_d(0, 1, 0, 3)
-        copy_d("s", 0, 0, 3)
-        copy_d("s", 0, 1, 0)
-        q_hul(1, 0, 256, 13)
-        turn_d(0, 1, 3, 1)
-        copy_d("s", 0, 1, 3)
-        il_e("v", 1, 0, 512, 16)
-        copy_d("s", 0, 0, 2)
-        il_d("g", 0, 0, 256, 512, 13)
-        turn_d(0, 1, 1, 2)
-        turn_d(0, 1, 2, 4)
-        q_e(1, 0, 512, 16)
-        copy_d("s", 0, 1, 1)
-        back_product(1, 0, 1, 3)
-        q_hul(1, 768, 1024, 15)
-        back_product(1, 0, 3, 6)
-        copy_d("s", 0, 1, 2)
-        store_d(0, 0, 2, 4)
-        store_d(0, 1, 0, 2)
-        back_product(1, 0, 2, 0)
-        subtract(1, 0, 1, 0, 4)
-        back_product(1, 0, 0, 5)
-        subtract(1, 0, 2, 0, 4)
-        il_d("g", 0, 1, 0, 256, 15)
-        back_product(1, 1, 3, 7)
-        il_d("s", 0, 0, 0, 256, 18)
-        subtract(1, 0, 3, 0, 4)
-        subtract(1, 0, 0, 0, 4)
-        back_product(1, 1, 0, 2)
-        back_product(1, 1, 1, 1)
-        subtract(1, 1, 1, 0, 2)
-        q_d(0, 0, 0, 256, 18)
-        back_product(1, 1, 2, 4)
-        q_d(0, 0, 256, 512, 13)
-        q_d(0, 1, 0, 256, 15)
-        il_d("s", 0, 1, 256, 512, 21)
-        turn_d(1, 0, 1, 0)
-        q_d(0, 1, 256, 512, 21)
-        turn_d(1, 0, 0, 6)
-        subtract(1, 1, 3, 0, 2)
-        turn_d(1, 0, 3, 5)
-        turn_d(1, 0, 2, 3)
-        store_d(0, 1, 2, 4)
-        copy_d("s", 1, 0, 1)
-        copy_d("s", 1, 0, 0)
-        store_codes(0, 0)
-        subtract(1, 1, 2, 0, 2)
-        store_codes(0, 1)
+        q_hul(1, 0, *LOW)
+        il_hul(gpsimd, 1, 1, *HIGH, reuse=True)
+        for r in (1, 2, 3):
+            subtract(0, 1, r)
+
+        copy_d(scalar, 0, 0, 0)
+        for r in SLOTS:
+            scale_e(1, r)
+        for t, b in ((1, 4), (2, 5), (3, 0)):
+            turn_d(0, 0, t, b)
+        copy_d(scalar, 0, 0, 1)
+        store_d(0, 0, 0)
+        copy_d(scalar, 0, 0, 2)
+        copy_d(scalar, 0, 0, 3)
+        store_d(0, 0, 1)
+        q_hul(1, 0, *HIGH)
+        q_hul(1, 1, *LOW)
+        q_hul(1, 1, *HIGH)
+        il_e(vector, 1)
+        q_e(1, *LOW)
+        q_e(1, *HIGH)
+        il_d(gpsimd, 0, 0, *LOW, reuse=True)
+        for t, b in enumerate((7, 2, 1, 3)):
+            turn_d(0, 1, t, b)
+        copy_d(vector, 0, 1, 3)
+        copy_d(scalar, 0, 1, 2)
+        store_d(0, 1, 1)
+        copy_d(scalar, 0, 1, 0)
+        copy_d(scalar, 0, 1, 1)
+        store_d(0, 1, 0)
+        il_d(gpsimd, 0, 1, *LOW)
+        il_d(scalar, 0, 0, *HIGH)
+        il_d(scalar, 0, 1, *HIGH)
+
+        banks_g0, banks_g1 = (6, 4, 5, 0), (3, 1, 7, 2)
+        for g, banks in enumerate((banks_g0, banks_g1)):
+            for r in SLOTS:
+                second_product(1, g, r, banks[r])
+        for r in SLOTS:
+            subtract(1, 0, r)
         subtract(1, 1, 0, 0, 2)
-        copy_d("s", 1, 0, 3)
-        copy_d("s", 1, 0, 2)
-        subtract(1, 1, 1, 2, 4)
-        turn_d(1, 1, 1, 6)
-        store_d(1, 0, 0, 2)
-        subtract(1, 1, 0, 2, 4)
-        subtract(1, 1, 2, 2, 4)
-        subtract(1, 1, 3, 2, 4)
-        copy_d("s", 1, 1, 1)
-        turn_d(1, 1, 0, 3)
-        turn_d(1, 1, 2, 4)
-        il_d("v", 1, 0, 0, 512, 22)
-        copy_d("s", 1, 1, 0)
-        copy_d("s", 1, 1, 2)
-        turn_d(1, 1, 3, 0)
-        store_d(1, 0, 2, 4)
-        q_d(1, 0, 0, 512, 22)
-        copy_d("s", 1, 1, 3)
-        il_d("v", 1, 1, 0, 256, 24)
-        q_d(1, 1, 0, 256, 24)
-        store_d(1, 1, 0, 2)
+        q_d(0, 0, *LOW)
+        q_d(0, 0, *HIGH)
+        store_codes(0, 0)
+        q_d(0, 1)
+        store_codes(0, 1)
+        for pair in range(2):
+            for t in (2 * pair, 2 * pair + 1):
+                turn_d(1, 0, t, banks_g0[t])
+                copy_d(scalar, 1, 0, t)
+            store_d(1, 0, pair)
+        for r in (1, 2, 3):
+            subtract(1, 1, r, 0, 2)
+        for r in SLOTS:
+            subtract(1, 1, r, 2, 4)
+        for t in (0, 1):
+            turn_d(1, 1, t, banks_g0[t])
+            copy_d(scalar, 1, 1, t)
+        store_d(1, 1, 0)
+        il_d(vector, 1, 0)
+        q_d(1, 0)
         store_codes(1, 0)
-        store_d(1, 1, 2, 4)
-        il_d("s", 1, 1, 256, 512, 25)
-        q_d(1, 1, 256, 512, 25)
+        for t in (2, 3):
+            turn_d(1, 1, t, banks_g0[t])
+            copy_d(scalar, 1, 1, t)
+        store_d(1, 1, 1)
+        il_d(vector, 1, 1, *LOW)
+        il_d(scalar, 1, 1, *HIGH)
+        q_d(1, 1)
         store_codes(1, 1)
-        store_scales(0, 2)
+        store_scales()

from contextlib import ExitStack

import concourse.mybir as mybir
from concourse.masks import make_identity

F, K, N = 2, 512, 1024
FLOPS = 2 * F * 2 * K * K * N

F32 = mybir.dt.float32
BF16 = mybir.dt.bfloat16
I32 = mybir.dt.int32
U32 = mybir.dt.uint32
U8 = mybir.dt.uint8
FP8X4 = mybir.dt.float8_e4m3fn_x4
ALU = mybir.AluOpType
ACT = mybir.ActivationFunctionType

P = 128
PASS = 512
G = N // PASS
HALF = PASS // 2
SLOTS = range(4)
C_ON_TENSOR = [(0, 0), (0, 1), (0, 2), (0, 3), (1, 0), (1, 1)]
STAGE_COLUMNS = 13 * PASS
NOISE, ONE, C_VECTOR, C_TENSOR, POWER, N_TERMS = 0, 1, 2, 3, 4, 5


def tile_wmmseunmatcheduplinkgradientsurrogate_kernel(tc, h, v, hul, u, a, s2, out_0, out_1, out_2):
    nc = tc.nc
    vector, scalar, gpsimd = nc.vector, nc.scalar, nc.gpsimd
    with ExitStack() as ctx:
        sb = ctx.enter_context(tc.tile_pool(name="sb", bufs=1))
        ps = ctx.enter_context(tc.psum_pool(name="ps", bufs=1))
        ctx.enter_context(tc.manual_schedule())

        def per_f(name, shape, dtype):
            return [sb.tile(shape, dtype, name=f"{name}{f}", align_bytes=64) for f in range(F)]

        ident = sb.tile([P, P], F32, name="ident")
        rows = sb.tile([P, K], BF16, name="rows")
        vec = sb.tile([P, 3, F, 4], F32, name="vec")
        usq = sb.tile([P, F, 4], F32, name="usq")
        m2u = sb.tile([P, F, 4], F32, name="m2u")
        coef = sb.tile([P, F, 2, 4], F32, name="coef")
        terms = sb.tile([P, F, 4, 8], F32, name="terms")
        mse = per_f("mse", [P, 4], F32)
        weight = per_f("weight", [P, 4], F32)
        gains = per_f("gains", [P, 2, 4], F32)
        junk_v = sb.tile([P, 4, HALF], F32, name="junk_v")
        junk_s = sb.tile([P, 2, K], BF16, name="junk_s")

        h_sb = per_f("h_sb", [P, 4, N], BF16)
        v_sb = per_f("v_sb", [P, G, 4, K], BF16)
        hul_sb = per_f("hul_sb", [P, G, 4, PASS], BF16)
        h_il = per_f("h_il", [P, 2, G, HALF, 4], BF16)
        e_raw = per_f("e_raw", [P, 4, K], BF16)
        stage = sb.tile([P, STAGE_COLUMNS, 4], BF16, name="stage", align_bytes=64)
        h_q, h_s = per_f("h_q", [P, 2, G, HALF], U32), per_f("h_s", [P, 2, G, HALF], U8)
        v_q, v_s = per_f("v_q", [P, G, K], U32), per_f("v_s", [P, G, K], U8)
        hul_q, hul_s = per_f("hul_q", [P, N], U32), per_f("hul_s", [P, N], U8)
        e_q, e_s = per_f("e_q", [P, K], U32), per_f("e_s", [P, K], U8)
        d_q = per_f("d_q", [P, G, K], U32)
        d_s = sb.tile([P, G, F * K], U8, name="d_s", align_bytes=64)

        live = {}
        home = {}
        staged = {}
        last_read = [0]

        def bank(b, *key):
            live[key] = ps.tile([P, PASS], F32, name="_".join(map(str, key)), tag=f"bank{b}")
            return live[key]

        def block(n):
            return slice(P * n, P * (n + 1))

        def copy(eng, out, in_):
            if eng is vector:
                vector.tensor_copy(out=out, in_=in_)
            else:
                scalar.copy(out=out, in_=in_)

        def quantize(codes, scales, src):
            vector.quantize_mx(out=codes.bitcast(FP8X4), scales=scales, in_=src.rearrange("p c t -> p (c t)"))

        def interleave(eng, operand, src, lo, hi, reuse):
            if reuse:
                first = last_read[0]
            else:
                first = home.setdefault(operand, PASS * len(home)) + lo
            for col in range(lo, hi, HALF):
                staged[operand, col] = first + col - lo
            dst, src = stage[:, first : first + hi - lo, :], src[:, :, lo:hi]
            if eng is gpsimd:
                gpsimd.tensor_scalar(out=dst, in0=src.rearrange("p t c -> p c t"), scalar1=1.0, scalar2=0.0,
                                     op0=ALU.mult, op1=ALU.add)
            else:
                copy(eng, dst.rearrange("p (c x) t -> p c t x", x=4), src.rearrange("p t (c x) -> p c t x", x=4))

        def quantize_staged(operand, codes, scales, lo, hi):
            first = staged[operand, lo]
            last_read[0] = first
            quantize(codes[:, lo:hi], scales[:, lo:hi], stage[:, first : first + hi - lo, :])

        def load_v(f, g):
            nc.sync.dma_start(out=v_sb[f][:, g], in_=v[f, PASS * g : PASS * (g + 1), :].rearrange("(i t) j -> i t j", t=4))

        def load_h(f, pair):
            users = slice(2 * pair, 2 * pair + 2)
            nc.sync.dma_start(out=h_sb[f][:, users, :], in_=h[f].rearrange("(m r) n -> m r n", r=4)[:, users, :])

        def load_hul(f, g):
            antennas = slice(PASS * g, PASS * (g + 1))
            nc.sync.dma_start(out=hul_sb[f][:, g], in_=hul[f].rearrange("(m r) n -> m r n", r=4)[:, :, antennas])

        def load_vectors():
            gpsimd.memset(rows[:].bitcast(F32), 0.0)
            for n, src in enumerate((u, a, s2)):
                nc.sync.dma_start(out=rows[F * n : F * (n + 1), :], in_=src)

        def turn_vectors(b):
            acc = bank(b, "vectors")
            words = rows[:].bitcast(F32)
            for x in range(2):
                nc.tensor.transpose(acc[:, block(x)], words[:, x::2], ident[:])

        def unpack_vectors():
            turned = live["vectors",][:, : 2 * P].bitcast(BF16).rearrange("p (x row y) -> p row x y", x=2, y=2)
            scalar.activation(out=usq[:].rearrange("p f (x y) -> p f x y", x=2), in_=turned[:, :F], func=ACT.Square)
            scalar.copy(out=vec[:].rearrange("p n f (x y) -> p (n f) x y", x=2), in_=turned[:, : 3 * F])

        def user_terms():
            vector.memset(terms[:, :, :, ONE], 1.0)
            vector.tensor_scalar(out=m2u[:], in0=vec[:, 0], scalar1=-2.0, scalar2=None, op0=ALU.mult)
            vector.scalar_tensor_tensor(out=coef[:, :, 1, :], in0=vec[:, 1], scalar=-1.0, in1=vec[:, 0],
                                        op0=ALU.mult, op1=ALU.mult)
            vector.tensor_tensor(out=coef[:, :, 0, :], in0=vec[:, 1], in1=usq[:], op=ALU.mult)
            vector.tensor_tensor(out=terms[:, :, :, NOISE], in0=vec[:, 2], in1=usq[:], op=ALU.mult)

        def il_v(eng, f, g, lo=0, hi=PASS, reuse=False):
            interleave(eng, ("v", f, g), v_sb[f][:, g], lo, hi, reuse)

        def q_v(f, g, lo=0, hi=PASS):
            quantize_staged(("v", f, g), v_q[f][:, g, :], v_s[f][:, g, :], lo, hi)

        def turn_h(f, pair, g, b):
            acc = bank(b, "hT", f, pair, g)
            for rr in range(2):
                words = h_sb[f][:, 2 * pair + rr, :].bitcast(F32)
                for x in range(2):
                    nc.tensor.transpose(acc[:, block(2 * rr + x)], words[:, HALF * g + x : HALF * (g + 1) : 2], ident[:])

        def copy_h(f, pair, g):
            words = h_il[f][:, pair, g].rearrange("p k t -> p (k t)").bitcast(F32)
            scalar.copy(out=words.rearrange("p (r m x) -> p r m x", r=2, x=2),
                        in_=live["hT", f, pair, g][:].rearrange("p (r x m) -> p r m x", r=2, x=2))

        def q_h(f, pair, g_lo=0, g_hi=G):
            quantize(h_q[f][:, pair, g_lo:g_hi].rearrange("p g c -> p (g c)"),
                     h_s[f][:, pair, g_lo:g_hi].rearrange("p g c -> p (g c)"),
                     h_il[f][:, pair, g_lo:g_hi].rearrange("p g c t -> p (g c) t"))

        def turn_v(f, b):
            acc = bank(b, "vT", f)
            for tt in range(2):
                words = v_sb[f][:, 1, 2 + tt, :].bitcast(F32)
                for x in range(2):
                    nc.tensor.transpose(acc[:, block(2 * tt + x)], words[:, x::2], ident[:])

        def c_vector(f, r):
            v_turned = live["vT", f][:].bitcast(BF16).rearrange("p (t x i y) -> p t x i y", t=2, x=2, y=2)
            h_row = h_sb[f][:, r, PASS:].rearrange("p (i t) -> p t i", t=4)
            vector.scalar_tensor_tensor(
                out=junk_v[:, r, :].rearrange("p (t i) -> p t i", t=2), in0=v_turned[:, :, r // 2, :, r % 2],
                scalar=m2u[:, f, r : r + 1], in1=h_row[:, 2:4, :], op0=ALU.mult, op1=ALU.mult,
                accum_out=terms[:, f, r, C_VECTOR : C_VECTOR + 1])

        def c_tensor(f, r, b):
            acc = bank(b, "c", f) if r == 0 else live["c", f]
            for n, (g, t) in enumerate(C_ON_TENSOR):
                nc.tensor.matmul(acc[:, block(r)], lhsT=h_il[f][:, r // 2, g, block(r % 2), t],
                                 rhs=v_sb[f][:, g, t, r::4], start=n == 0, stop=n == len(C_ON_TENSOR) - 1)

        def c_diagonal(f, r):
            vector.scalar_tensor_tensor(
                out=junk_v[:, r, :P], in0=live["c", f][:, block(r)], scalar=m2u[:, f, r : r + 1], in1=ident[:],
                op0=ALU.mult, op1=ALU.mult, accum_out=terms[:, f, r, C_TENSOR : C_TENSOR + 1])

        def first_product(f, r, b):
            acc = bank(b, "p", f, r)
            for g in range(G):
                nc.tensor.matmul_mx(out=acc[:], lhsT=h_q[f][:, r // 2, g, block(r % 2)].bitcast(FP8X4),
                                    lhsT_scale=h_s[f][:, r // 2, g, block(r % 2)],
                                    rhs=v_q[f][:, g, :].bitcast(FP8X4), rhs_scale=v_s[f][:, g, :],
                                    start=g == 0, stop=g == G - 1)

        def power(f, r):
            scalar.activation(out=junk_s[:, r % 2, :], in_=live["p", f, r][:], func=ACT.Square,
                              scale=vec[:, 0, f, r : r + 1], accum_out=terms[:, f, r, POWER : POWER + 1])

        def weights_sum(f):
            vector.tensor_reduce(out=mse[f][:], in_=terms[:, f, :, :N_TERMS], axis=mybir.AxisListType.X, op=ALU.add)

        def weights_inverse(f):
            vector.reciprocal(out=weight[f][:], in_=mse[f][:])

        def weights_gains(f):
            vector.tensor_tensor(out=gains[f][:], in0=coef[:, f], in1=weight[f][:].unsqueeze(1).to_broadcast([P, 2, 4]),
                                 op=ALU.mult)

        def scale_e(f, r):
            scalar.activation(out=e_raw[f][:, r, :].rearrange("p (s m) -> p s m", s=4),
                              in_=live["p", f, r][:].rearrange("p (m s) -> p s m", s=4),
                              func=ACT.Copy, scale=gains[f][:, 0, r : r + 1])

        def il_e(eng, f, lo=0, hi=PASS):
            interleave(eng, ("e", f), e_raw[f][:], lo, hi, False)

        def q_e(f, lo, hi):
            quantize_staged(("e", f), e_q[f][:], e_s[f][:], lo, hi)

        def il_hul(eng, f, g, lo=0, hi=PASS, reuse=False):
            interleave(eng, ("hul", f, g), hul_sb[f][:, g], lo, hi, reuse)

        def q_hul(f, g, lo, hi):
            antennas = slice(PASS * g, PASS * (g + 1))
            quantize_staged(("hul", f, g), hul_q[f][:, antennas], hul_s[f][:, antennas], lo, hi)

        def second_product(f, g, r, b):
            acc = bank(b, "d1T", f, g, r)
            antennas = slice(PASS * g, PASS * (g + 1))
            nc.tensor.matmul_mx(out=acc[:], lhsT=e_q[f][:, block(r)].bitcast(FP8X4), lhsT_scale=e_s[f][:, block(r)],
                                rhs=hul_q[f][:, antennas].bitcast(FP8X4), rhs_scale=hul_s[f][:, antennas],
                                start=True, stop=True)

        def subtract(f, g, r, t_lo=0, t_hi=4):
            if ("dT", f, g) not in live:
                tag = f"dT{g}" if f == 0 else f"h_il{g}"
                live["dT", f, g] = sb.tile([P, 4, PASS], F32, name=f"dT{f}{g}", tag=tag, align_bytes=64)
            vector.scalar_tensor_tensor(
                out=live["dT", f, g][:, r, :].rearrange("p (t i) -> p t i", t=4)[:, t_lo:t_hi],
                in0=hul_sb[f][:, g, r, :].rearrange("p (i t) -> p t i", t=4)[:, t_lo:t_hi],
                scalar=gains[f][:, 1, r : r + 1],
                in1=live["d1T", f, g, r][:].rearrange("p (i t) -> p t i", t=4)[:, t_lo:t_hi],
                op0=ALU.mult, op1=ALU.add)

        def turn_d(f, g, t, b):
            acc = bank(b, "d", f, g, t)
            for r in SLOTS:
                nc.tensor.transpose(acc[:, block(r)], live["dT", f, g][:, r, block(t)], ident[:])

        def copy_d(eng, f, g, t):
            if ("d_sb", f, g) not in live:
                live["d_sb", f, g] = sb.tile([P, 4, K], F32, name=f"d_sb{f}{g}")
            copy(eng, live["d_sb", f, g][:, t, :].rearrange("p (m r) -> p m r", r=4),
                 live["d", f, g, t][:].rearrange("p (r m) -> p m r", r=4))

        def store_d(f, g, pair):
            slots = slice(2 * pair, 2 * pair + 2)
            dst = out_0[f, PASS * g : PASS * (g + 1), :].rearrange("(i t) j -> i t j", t=4)
            nc.sync.dma_start(out=dst[:, slots, :], in_=live["d_sb", f, g][:, slots, :])

        def il_d(eng, f, g, lo=0, hi=PASS, reuse=False):
            interleave(eng, ("d", f, g), live["d_sb", f, g][:], lo, hi, reuse)

        def q_d(f, g, lo=0, hi=PASS):
            quantize_staged(("d", f, g), d_q[f][:, g, :], d_s[:, g, K * f : K * (f + 1)], lo, hi)

        def store_codes(f, g):
            words = out_1[g].rearrange("p m t -> p (m t)").bitcast(I32)
            nc.sync.dma_start(out=words[:, K * f : K * (f + 1)], in_=d_q[f][:, g, :].bitcast(I32))

        def store_scales():
            for q, queue in enumerate((nc.sync, scalar, nc.sync, scalar)):
                dst = out_2[:, 4 * q : 4 * q + 4, :].rearrange("g row m -> row g m")
                queue.dma_start(out=dst.bitcast(I32), in_=d_s[32 * q : 32 * q + 4].bitcast(I32))

        LOW, HIGH = (0, HALF), (HALF, PASS)

        load_v(0, 1)
        load_vectors()
        load_h(0, 0)
        load_h(0, 1)
        load_v(0, 0)
        load_v(1, 1)
        load_hul(0, 0)
        load_v(1, 0)
        load_h(1, 0)
        load_h(1, 1)
        load_hul(0, 1)
        load_hul(1, 0)
        load_hul(1, 1)
        make_identity(nc, ident[:])

        turn_vectors(7)
        unpack_vectors()
        turn_v(0, 6)
        il_v(vector, 0, 1, *LOW)
        il_v(scalar, 0, 1, *HIGH)
        user_terms()
        q_v(0, 1, *LOW)
        c_vector(0, 0)
        c_vector(0, 1)
        q_v(0, 1, *HIGH)
        c_vector(0, 2)
        for pair in range(2):
            for g in range(G):
                turn_h(0, pair, g, 2 * pair + g)
                copy_h(0, pair, g)
        q_h(0, 0)
        il_v(vector, 0, 0)
        q_h(0, 1)
        q_v(0, 0)
        for r in SLOTS:
            c_tensor(0, r, 4)
        il_v(scalar, 1, 1)
        for r in SLOTS:
            first_product(0, r, r)
            power(0, r)
        il_hul(vector, 0, 0)
        q_hul(0, 0, *LOW)
        il_v(gpsimd, 1, 0, *LOW, reuse=True)
        c_vector(0, 3)
        for r in SLOTS:
            c_diagonal(0, r)
        q_hul(0, 0, *HIGH)
        il_v(vector, 1, 0, *HIGH)

        for pair, g, b in ((0, 0, 5), (0, 1, 7), (1, 0, 4)):
            turn_h(1, pair, g, b)
            copy_h(1, pair, g)
        turn_h(1, 1, 1, 6)
        turn_v(1, 5)
        weights_sum(0)
        q_v(1, 1, *LOW)
        weights_inverse(0)
        q_v(1, 1, *HIGH)
        weights_gains(0)
        q_h(1, 0)
        q_v(1, 0, *LOW)
        q_v(1, 0, *HIGH)
        il_hul(gpsimd, 0, 1, *LOW, reuse=True)
        for r in SLOTS:
            scale_e(0, r)
        copy_h(1, 1, 1)
        c_tensor(1, 0, 7)
        first_product(1, 0, 4)
        first_product(1, 1, 0)
        c_tensor(1, 1, 7)
        c_tensor(1, 2, 7)
        for r in SLOTS:
            c_vector(1, r)
        q_h(1, 1, 0, 1)
        il_e(vector, 0, *LOW)
        il_e(scalar, 0, *HIGH)
        q_h(1, 1, 1, 2)
        q_e(0, *LOW)
        q_e(0, *HIGH)
        il_hul(gpsimd, 1, 0, *LOW, reuse=True)

        second_product(0, 0, 0, 1)
        second_product(0, 0, 1, 2)
        first_product(1, 2, 3)
        first_product(1, 3, 6)
        second_product(0, 0, 2, 5)
        power(1, 0)
        il_hul(scalar, 0, 1, *HIGH)
        for r in (1, 2, 3):
            power(1, r)
        il_hul(scalar, 1, 0, *HIGH)
        for r in (0, 1, 2):
            c_diagonal(1, r)
        c_tensor(1, 3, 7)
        subtract(0, 0, 0)
        second_product(0, 0, 3, 1)
        subtract(0, 0, 1)
        q_hul(0, 1, *LOW)
        q_hul(0, 1, *HIGH)
        il_hul(gpsimd, 1, 1, *LOW, reuse=True)
        second_product(0, 1, 0, 2)
        subtract(0, 0, 2)
        second_product(0, 1, 1, 5)
        c_diagonal(1, 3)
        second_product(0, 1, 2, 7)
        subtract(0, 0, 3)
        turn_d(0, 0, 0, 1)
        weights_sum(1)
        subtract(0, 1, 0)
        second_product(0, 1, 3, 2)
        weights_inverse(1)
        weights_gains(1)
        q_hul(1, 0, *LOW)
        il_hul(gpsimd, 1, 1, *HIGH, reuse=True)
        for r in (1, 2, 3):
            subtract(0, 1, r)

        copy_d(scalar, 0, 0, 0)
        for r in SLOTS:
            scale_e(1, r)
        for t, b in ((1, 4), (2, 5), (3, 0)):
            turn_d(0, 0, t, b)
        copy_d(scalar, 0, 0, 1)
        store_d(0, 0, 0)
        copy_d(scalar, 0, 0, 2)
        copy_d(scalar, 0, 0, 3)
        store_d(0, 0, 1)
        q_hul(1, 0, *HIGH)
        q_hul(1, 1, *LOW)
        q_hul(1, 1, *HIGH)
        il_e(vector, 1)
        q_e(1, *LOW)
        q_e(1, *HIGH)
        il_d(gpsimd, 0, 0, *LOW, reuse=True)
        for t, b in enumerate((7, 2, 1, 3)):
            turn_d(0, 1, t, b)
        copy_d(vector, 0, 1, 3)
        copy_d(scalar, 0, 1, 2)
        store_d(0, 1, 1)
        copy_d(scalar, 0, 1, 0)
        copy_d(scalar, 0, 1, 1)
        store_d(0, 1, 0)
        il_d(gpsimd, 0, 1, *LOW)
        il_d(scalar, 0, 0, *HIGH)
        il_d(scalar, 0, 1, *HIGH)

        banks_g0, banks_g1 = (6, 4, 5, 0), (3, 1, 7, 2)
        for g, banks in enumerate((banks_g0, banks_g1)):
            for r in SLOTS:
                second_product(1, g, r, banks[r])
        for r in SLOTS:
            subtract(1, 0, r)
        subtract(1, 1, 0, 0, 2)
        q_d(0, 0, *LOW)
        q_d(0, 0, *HIGH)
        store_codes(0, 0)
        q_d(0, 1)
        store_codes(0, 1)
        for pair in range(2):
            for t in (2 * pair, 2 * pair + 1):
                turn_d(1, 0, t, banks_g0[t])
                copy_d(scalar, 1, 0, t)
            store_d(1, 0, pair)
        for r in (1, 2, 3):
            subtract(1, 1, r, 0, 2)
        for r in SLOTS:
            subtract(1, 1, r, 2, 4)
        for t in (0, 1):
            turn_d(1, 1, t, banks_g0[t])
            copy_d(scalar, 1, 1, t)
        store_d(1, 1, 0)
        il_d(vector, 1, 0)
        q_d(1, 0)
        store_codes(1, 0)
        for t in (2, 3):
            turn_d(1, 1, t, banks_g0[t])
            copy_d(scalar, 1, 1, t)
        store_d(1, 1, 1)
        il_d(vector, 1, 1, *LOW)
        il_d(scalar, 1, 1, *HIGH)
        q_d(1, 1)
        store_codes(1, 1)
        store_scales()
